import numpy as np
import ml_dtypes


def mxq(x, axis, fmt="e4m3"):
    dtype, down = {"e4m3": (ml_dtypes.float8_e4m3fn, 7), "e5m2": (ml_dtypes.float8_e5m2, 14)}[fmt]
    v = np.moveaxis(np.asarray(x, np.float32).astype(ml_dtypes.bfloat16).astype(np.float64), axis, -1)
    blocks = v.reshape(v.shape[:-1] + (-1, 32))
    amax = np.abs(blocks).max(-1, keepdims=True)
    byte = np.maximum(np.where(amax > 0, np.frexp(amax)[1] - 1 + 127, 0) - down, 1)
    scale = np.exp2(byte - 127.0)
    codes = (blocks / scale).astype(np.float32).astype(dtype).astype(np.float64)
    return np.moveaxis((codes * scale).reshape(v.shape), -1, axis)


WIDE = False


def mx_kscale(k):
    if not WIDE:
        return np.ones(k)
    levels = np.array([10, -10, 5, -5, 0])
    if k % 512:
        return np.exp2(np.random.permutation(np.resize(levels, k // 32))).repeat(32)
    a = np.empty((k // 512, 16))
    for p in range(k // 512):
        a[p, :8] = np.random.permutation(np.resize(levels, 8))
        for g in range(8):
            far = levels[np.abs(levels - a[p, g]) >= 10]
            a[p, g + 8] = far[np.random.randint(len(far))]
    return np.exp2(a.ravel()).repeat(32)


BF16 = ml_dtypes.bfloat16


def bf(x):
    return np.asarray(x, np.float32).astype(BF16)


def f64(x):
    return np.asarray(x).astype(np.float64)

def planes(Y):
    n, m = Y.shape
    b = f64(bf(Y)).reshape(n // 32, 32, m)
    amax = np.abs(b).max(1)
    byte = np.clip(np.where(amax > 0, np.frexp(amax)[1] - 1 + 127 - 7, 1), 1, 254)
    codes = (b * np.exp2(127.0 - byte)[:, None, :]).reshape(n, m).astype(np.float32).astype(ml_dtypes.float8_e4m3fn).view(np.uint8)
    words = codes.reshape(n // 512, 128, 4, m).transpose(0, 1, 3, 2)
    return np.ascontiguousarray(words), np.ascontiguousarray(byte.astype(np.uint8).reshape(n // 512, 16, m))


H, N, G, P, D = 2, 512, 4, 512, 512
T = G * P


def setup_inputs():
    s, t = mx_kscale(D), mx_kscale(T)
    return {
        "q": bf(np.random.standard_normal((H, N, D)) * 1.5),
        "k_code": bf(np.random.uniform(-1.5, 1.5, (H, G, P, D)) / s),
        "k_scale": bf(np.random.uniform(0.5, 1.5, (H, G, D)) * s),
        "k_zero": bf(np.random.standard_normal((H, G, D)) * 0.3),
        "v_code": bf(np.random.uniform(-3.0, 3.0, (H, T, D)) / t[None, :, None]),
        "v_scale": bf(np.random.standard_normal((H, T)) * 2.0 * t),
    }


def grouped_scores(q, k_code, k_scale, k_zero):
    qs = q[:, None, :, :] * k_scale[:, :, None, :]
    off = np.sum(q[:, None, :, :] * k_zero[:, :, None, :], axis=-1)
    a = mxq(qs, 3, "e4m3") @ mxq(k_code, 3, "e4m3").transpose(0, 1, 3, 2)
    return (a + off[..., None]) / np.sqrt(D)


def core(q, k_code, k_scale, k_zero, v_code, v_scale):
    sc = grouped_scores(f64(q), f64(k_code), f64(k_scale), f64(k_zero))
    sc = sc.transpose(0, 2, 1, 3).reshape(H, N, T)
    e = np.exp(sc - sc.max(axis=-1, keepdims=True))
    w = e / e.sum(axis=-1, keepdims=True)
    ws = w * f64(v_scale)[:, None, :]
    return mxq(ws, 2, "e4m3") @ mxq(f64(v_code), 1, "e4m3")


def reference(q, k_code, k_scale, k_zero, v_code, v_scale):
    R_out = core(q, k_code, k_scale, k_zero, v_code, v_scale)
    words, scales = planes(np.moveaxis(R_out, 1, 0).reshape(512, -1))
    return R_out, words, scales

@@ -1,0 +1,417 @@
+from contextlib import ExitStack
+
+import concourse.mybir as mybir
+from concourse.masks import make_identity
+
+H, N, G, T, D = 2, 512, 4, 2048, 512
+FLOPS = 2 * 2 * H * N * T * D
+
+F32 = mybir.dt.float32
+BF16 = mybir.dt.bfloat16
+I32 = mybir.dt.int32
+U32 = mybir.dt.uint32
+U8 = mybir.dt.uint8
+FP8X4 = mybir.dt.float8_e4m3fn_x4
+ALU = mybir.AluOpType
+ACT = mybir.ActivationFunctionType
+
+P = 128
+PACK = 4
+W = 512
+SOFTMAX_SCALE = D ** -0.5
+
+
+def pieces(h, i):
+    if (h, i) == (H - 1, PACK - 1):
+        return [(0, 2), (2, 3), (3, 4)]
+    return [(0, 2), (2, 4)]
+
+
+def engine_orders():
+    pe, act, dve = [], [], []
+    both = (0, 1)
+
+    def each(name, h, i):
+        return [(name, h, i) + piece for piece in pieces(h, i)]
+
+    pe += [("tq", 0, 0), ("tz",), ("tq", 0, 1), ("tk", 0, 0, 0), ("tk", 0, 0, 1), ("tk", 0, 1, 0), ("off", 0), ("tk", 0, 1, 1)]
+    act += [("cq", 0, 1), ("ck", 0, 0, 0), ("ck", 0, 0, 1), ("ck", 0, 1, 0), ("coff", 0), ("ck", 0, 1, 1)]
+    dve += [("cq", 0, 0), ("cz",), ("mq", 0, 0), ("qk", 0, 0), ("qq", 0, 0)]
+    for h in range(H):
+        first, last = h == 0, h == H - 1
+        for g in range(G):
+            if first and g == 0:
+                pe += [("ms", h, g, 0), ("ms", h, g, 1), ("ms", h, g, 2), ("tk", h, 2, 0), ("ms", h, g, 3), ("tk", h, 2, 1)]
+            elif g == 0:
+                pe += [("ms", h, g, 0), ("ms", h, g, 1), ("ms", h, g, 2), ("tk", h, 2, 0)] + each("mo", h - 1, 2)
+                pe += [("ms", h, g, 3), ("tk", h, 2, 1)] + each("mo", h - 1, 3)
+            elif g == 1:
+                pe += [("ms", h, g, 0), ("ms", h, g, 1), ("ms", h, g, 2), ("tk", h, 3, 0), ("ms", h, g, 3), ("tk", h, 3, 1)]
+            else:
+                pe += [("ms", h, g, i) for i in range(PACK)]
+            if not last and g == 2:
+                pe += [("tq", h + 1, b) for b in both] + [("tk", h + 1, 0, 0)]
+            if not last and g == 3:
+                pe += [("tk", h + 1, 0, 1), ("off", h + 1)]
+            if g < G - 1:
+                dve += [("mq", h, g + 1), ("sp", h, g, 0), ("qq", h, g + 1), ("sp", h, g, 1)]
+                if not first and g == 0:
+                    dve += each("qw", h - 1, 3)
+                dve += [("qk", h, g + 1), ("sp", h, g, 2)]
+                if not first and g == 2:
+                    dve += [("qo", h - 1, c) for c in both]
+                dve += [("sp", h, g, 3)]
+        if first:
+            act += [("iv", h, 0, b) for b in both] + [("ck", h, 2, b) for b in both] + [("iv", h, 1, b) for b in both]
+            act += [("ck", h, 3, b) for b in both] + [("iv", h, g, b) for g in (2, 3) for b in both]
+        else:
+            act += [("ck", h, 2, 0), ("iv", h, 0, 1), ("co", h - 1, 2, 0), ("ck", h, 2, 1), ("iv", h, 1, 0), ("co", h - 1, 3, 0), ("iv", h, 1, 1)]
+            act += [("ck", h, 3, 0), ("ck", h, 3, 1), ("io", h - 1, 0), ("io", h - 1, 1)] + [("iv", h, g, b) for g in (2, 3) for b in both]
+        dve += [("sp", h, 3, 0), ("qv", h, 0), ("sp", h, 3, 1), ("qv", h, 1), ("sp", h, 3, 2), ("sp", h, 3, 3), ("rc", h, 0), ("qv", h, 2)]
+        dve += each("st", h, 0) + [("rc", h, 1), ("qv", h, 3)] + each("st", h, 1) + [("rc", h, 2)] + each("qw", h, 0)
+        dve += each("st", h, 2) + [("rc", h, 3)]
+        pe += each("tw", h, 0) + each("tw", h, 1) + each("mo", h, 0) + each("tw", h, 2)
+        if not last:
+            act += [("cq", h + 1, 0), ("cq", h + 1, 1), ("nb", h, 0), ("ck", h + 1, 0, 0)]
+            act += [("ex", h, 0), ("nb", h, 1), ("ck", h + 1, 0, 1), ("ex", h, 1), ("nb", h, 2), ("nb", h, 3), ("coff", h + 1), ("ex", h, 2)]
+            act += each("cw", h, 0) + [("ex", h, 3)] + each("cw", h, 1) + [("co", h, 0, 0)] + each("cw", h, 2)
+            act += [("ck", h + 1, 1, 0), ("ck", h + 1, 1, 1), ("co", h, 1, 0), ("iv", h + 1, 0, 0)] + each("cw", h, 3)
+            tail = each("st", h, 3)
+            dve += [("mq", h + 1, 0)] + each("qw", h, 1) + [("qk", h + 1, 0), tail[0], ("qq", h + 1, 0), tail[1]] + each("qw", h, 2)
+            pe += [("tk", h + 1, 1, b) for b in both] + each("mo", h, 1) + each("tw", h, 3)
+        else:
+            act += [("nb", h, 0), ("ex", h, 0), ("nb", h, 1), ("nb", h, 2), ("ex", h, 1), ("nb", h, 3), ("ex", h, 2)]
+            act += each("cw", h, 0) + [("ex", h, 3)] + each("cw", h, 1) + [("co", h, 0, 0)] + each("cw", h, 2)
+            act += each("cw", h, 3)[:1] + [("co", h, 1, 0)] + each("cw", h, 3)[1:] + [("co", h, 2, 0), ("co", h, 3, 0), ("co", h, 3, 1)]
+            dve += each("qw", h, 1) + each("st", h, 3)[:2] + each("qw", h, 2) + each("st", h, 3)[2:] + each("qw", h, 3)
+            dve += [("io", h, 0), ("io", h, 1), ("qo", h, 0), ("qo", h, 1)]
+            pe += each("mo", h, 1) + each("tw", h, 3)[:2] + each("mo", h, 2)[:1] + each("tw", h, 3)[2:] + each("mo", h, 2)[1:] + each("mo", h, 3)
+    return pe, act, dve
+
+
+def producers(step):
+    name, args = step[0], step[1:]
+    both = (0, 1)
+    table = {
+        "cz": lambda: [("tz",)],
+        "cq": lambda h, b: [("tq", h, b)],
+        "ck": lambda h, g, b: [("tk", h, g, b)],
+        "off": lambda h: [("cz",)] + [("cq", h, b) for b in both],
+        "coff": lambda h: [("off", h)],
+        "mq": lambda h, g: [("cz",)] + [("cq", h, b) for b in both],
+        "qq": lambda h, g: [("mq", h, g)],
+        "qk": lambda h, g: [("ck", h, g, b) for b in both],
+        "qv": lambda h, g: [("iv", h, g, b) for b in both],
+        "ms": lambda h, g, i: [("qq", h, g), ("qk", h, g)],
+        "sp": lambda h, g, i: [("ms", h, g, i), ("coff", h)],
+        "nb": lambda h, i: [("sp", h, G - 1, i)],
+        "ex": lambda h, i: [("nb", h, i)],
+        "rc": lambda h, i: [("ex", h, i)],
+        "st": lambda h, i, g0, g1: [("rc", h, i)],
+        "tw": lambda h, i, g0, g1: [("st", h, i, g0, g1)],
+        "cw": lambda h, i, g0, g1: [("tw", h, i, g0, g1)],
+        "qw": lambda h, i, g0, g1: [("cw", h, i, g0, g1)],
+        "mo": lambda h, i, g0, g1: [("qw", h, i, g0, g1)] + [("qv", h, g) for g in range(g0, g1)],
+        "co": lambda h, i, c: [("mo", h, i) + pieces(h, i)[-1]],
+        "io": lambda h, c: [("co", h, i, 0) for i in range(PACK - 1)] + [("co", h, PACK - 1, c if h == H - 1 else 0)],
+        "qo": lambda h, c: [("io", h, c)],
+    }
+    return table[name](*args) if name in table else []
+
+
+def schedule():
+    queues = [list(order) for order in engine_orders()]
+    written, text = set(), []
+    for turn in range(sum(len(order) for order in queues)):
+        ready = [order for order in queues if order and all(p in written for p in producers(order[0]))]
+        step = ready[0][0]
+        ready[0].remove(step)
+        written.add(step)
+        text.append(step)
+    return text
+
+
+def tile_kivigroupedscalefoldedattention_x1_kernel(tc, q, k_code, k_scale, k_zero, v_code, v_scale, out_0, out_1, out_2):
+    nc = tc.nc
+    with ExitStack() as ctx:
+        keep = ctx.enter_context(tc.tile_pool(name="keep", bufs=1))
+        stage = ctx.enter_context(tc.tile_pool(name="stage", bufs=3))
+        acc_pool = ctx.enter_context(tc.psum_pool(name="acc", bufs=3))
+        out_pool = ctx.enter_context(tc.psum_pool(name="out", bufs=1))
+        turn_pool = ctx.enter_context(tc.psum_pool(name="turn", bufs=4))
+        ctx.enter_context(tc.manual_schedule())
+
+        def kept(name, shape, dtype):
+            return keep.tile(shape, dtype, name=name, align_bytes=64)
+
+        def staged(tag, shape, dtype):
+            return stage.tile(shape, dtype, name=tag, tag=tag, align_bytes=64)
+
+        def per_head(tag, shape, dtype):
+            return stage.tile(shape, dtype, name=tag, tag=tag, bufs=4, align_bytes=64)
+
+        factor_rows = kept("factor_rows", [P, D], BF16)
+        nc.gpsimd.memset(factor_rows[:].bitcast(I32), 0)
+        ident = kept("ident", [P, P], F32)
+        make_identity(nc, ident[:])
+        warm = kept("warm", [P, 1], F32)
+        nc.scalar.activation(out=warm[:], in_=ident[:, 0:1], func=ACT.Exp)
+
+        q_rows, k_rows, v_rows, vs_rows = {}, {}, {}, {}
+
+        def load_q(h):
+            src = q[h].rearrange("(p j) d -> p j d", j=PACK)
+            for b in range(2):
+                q_rows[h, b] = kept("q_rows%d%d" % (h, b), [P, 2, D], BF16)
+                nc.sync.dma_start(out=q_rows[h, b][:], in_=src[:, 2 * b : 2 * b + 2, :])
+
+        def load_k(h, g):
+            src = k_code[h, g].rearrange("(r p) d -> p r d", p=P)
+            for b in range(2):
+                k_rows[h, g, b] = kept("k_rows%d%d%d" % (h, g, b), [P, 2, D], BF16)
+                nc.sync.dma_start(out=k_rows[h, g, b][:], in_=src[:, 2 * b : 2 * b + 2, :])
+
+        def load_v(h, g):
+            v_rows[h, g] = per_head("v_rows", [P, PACK, D], BF16)
+            nc.sync.dma_start(out=v_rows[h, g][:], in_=v_code[h, g * W : (g + 1) * W, :].rearrange("(p j) d -> p j d", j=PACK))
+
+        def load_vs(h):
+            vs_rows[h] = kept("vs_rows%d" % h, [P, T], BF16)
+            nc.sync.dma_start(out=vs_rows[h][:], in_=v_scale[h].partition_broadcast(P))
+
+        load_q(0)
+        nc.sync.dma_start(out=factor_rows[0 : H * G, :], in_=k_scale.rearrange("h g d -> (h g) d"))
+        nc.sync.dma_start(out=factor_rows[H * G : 2 * H * G, :], in_=k_zero.rearrange("h g d -> (h g) d"))
+        load_k(0, 0)
+        for h in range(H):
+            load_k(h, 1)
+            load_v(h, 0)
+            load_k(h, 2)
+            load_v(h, 1)
+            load_k(h, 3)
+            load_v(h, 2)
+            load_v(h, 3)
+            if h + 1 < H:
+                load_q(h + 1)
+                load_k(h + 1, 0)
+            load_vs(h)
+
+        factors = kept("factors", [P, 2 * H * G, PACK], BF16)
+        q_t = {h: kept("q_t%d" % h, [P, N, PACK], BF16) for h in range(H)}
+        offs = {h: kept("offs%d" % h, [P, PACK, G], F32) for h in range(H)}
+        run_max = {h: kept("run_max%d" % h, [P, PACK, G], F32) for h in range(H)}
+        exp_bias = {h: kept("exp_bias%d" % h, [P, PACK], F32) for h in range(H)}
+        row_sum = {h: kept("row_sum%d" % h, [P, PACK], F32) for h in range(H)}
+        row_inv = {h: kept("row_inv%d" % h, [P, PACK], F32) for h in range(H)}
+        scores = {}
+        result = {h: kept("result%d" % h, [P, PACK, D], F32) for h in range(H)}
+        live = {}
+
+        def words(tile_ap):
+            return tile_ap.bitcast(F32)
+
+        def turn(key, sources):
+            bank = turn_pool.tile([P, len(sources), 2, P], F32, name="turn_bank", tag="turn_bank")
+            for r, src in enumerate(sources):
+                for u in range(2):
+                    nc.tensor.transpose(bank[:, r, u, :], src[:, u : 2 * P : 2], ident[:])
+            live[key] = bank
+
+        def turn_out(key, dst, engine):
+            src = live[key][:].rearrange("p r u m -> p r m u")
+            view = dst.rearrange("p c j -> p (c j)").bitcast(F32).rearrange("p (r m u) -> p r m u", m=P, u=2)
+            if engine == "v":
+                nc.vector.tensor_copy(out=view, in_=src)
+            else:
+                nc.scalar.copy(out=view, in_=src)
+
+        def quantize(key, pool_fn, tag, src):
+            codes = pool_fn(tag + "_codes", [P, src.shape[1]], U32)
+            scales = pool_fn(tag + "_scales", [P, src.shape[1]], U8)
+            nc.vector.quantize_mx(out=codes[:].bitcast(FP8X4), scales=scales[:], in_=src.rearrange("p c j -> p (c j)"))
+            live[key] = (codes, scales)
+
+        def mx(out, stationary, cols, moving, moving_cols, start, stop):
+            nc.tensor.matmul_mx(
+                out=out,
+                lhsT=stationary[0][:, cols].bitcast(FP8X4),
+                lhsT_scale=stationary[1][:, cols],
+                rhs=moving[0][:, moving_cols].bitcast(FP8X4),
+                rhs_scale=moving[1][:, moving_cols],
+                start=start,
+                stop=stop,
+            )
+
+        def tz():
+            bank = out_pool.tile([P, 2, P], F32, name="out_bank", tag="out_bank")
+            for u in range(2):
+                nc.tensor.transpose(bank[:, u, :], words(factor_rows[:])[:, u : 2 * P : 2], ident[:])
+            live["z"] = bank
+
+        def cz():
+            nc.vector.tensor_copy(
+                out=factors[:].rearrange("p r j -> p (r j)").bitcast(F32).rearrange("p (r u) -> p r u", u=2),
+                in_=live["z"][:, :, 0 : 2 * H * G].rearrange("p u r -> p r u"),
+            )
+
+        def tq(h, b):
+            turn(("q", h, b), [words(q_rows[h, b][:, r, :]) for r in range(2)])
+
+        def cq(h, b):
+            turn_out(("q", h, b), q_t[h][:, 2 * P * b : 2 * P * (b + 1), :], "v" if (h, b) == (0, 0) else "s")
+
+        def tk(h, g, b):
+            turn(("k", h, g, b), [words(k_rows[h, g, b][:, r, :]) for r in range(2)])
+
+        def ck(h, g, b):
+            if b == 0:
+                live["kt", h, g] = staged("k_t", [P, W, PACK], BF16)
+            turn_out(("k", h, g, b), live["kt", h, g][:, 2 * P * b : 2 * P * (b + 1), :], "s")
+
+        def off(h):
+            bank = out_pool.tile([P, PACK, G], F32, name="out_bank", tag="out_bank")
+            first = H * G + h * G
+            for i in range(PACK):
+                for j in range(PACK):
+                    nc.tensor.matmul(
+                        bank[:, i, :],
+                        lhsT=q_t[h][:, i * P : (i + 1) * P, j],
+                        rhs=factors[:, first : first + G, j],
+                        start=(j == 0),
+                        stop=(j == PACK - 1),
+                    )
+            live["off", h] = bank
+
+        def coff(h):
+            nc.scalar.copy(out=offs[h][:], in_=live["off", h][:])
+
+        def mq(h, g):
+            qs = staged("qs", [P, N, PACK], BF16)
+            nc.vector.tensor_tensor(
+                out=qs[:], in0=q_t[h][:], in1=factors[:, h * G + g : h * G + g + 1, :].to_broadcast([P, N, PACK]), op=ALU.mult
+            )
+            live["qs", h, g] = qs
+
+        def qq(h, g):
+            quantize(("qq", h, g), staged, "qs", live["qs", h, g][:])
+
+        def qk(h, g):
+            quantize(("qk", h, g), staged, "k", live["kt", h, g][:])
+
+        def iv(h, g, b):
+            if b == 0:
+                live["vt", h, g] = per_head("v_t", [P, D, PACK], BF16)
+            cols = slice(b * D // 2, (b + 1) * D // 2)
+            nc.scalar.copy(
+                out=live["vt", h, g][:, cols, :].rearrange("p (c i) j -> p c j i", i=4),
+                in_=v_rows[h, g][:, :, cols].rearrange("p j (c i) -> p c j i", i=4),
+            )
+
+        def qv(h, g):
+            quantize(("qv", h, g), per_head, "v", live["vt", h, g][:])
+
+        def ms(h, g, i):
+            bank = acc_pool.tile([P, W], F32, name="acc_bank", tag="acc_bank")
+            mx(bank[:], live["qq", h, g], slice(i * P, (i + 1) * P), live["qk", h, g], slice(0, W), True, True)
+            live["s", h, g, i] = bank
+
+        def sp(h, g, i):
+            if g == 0:
+                scores[h, i] = per_head("scores", [P, T], F32)
+            nc.vector.tensor_scalar(
+                out=scores[h, i][:, g * W : (g + 1) * W],
+                in0=live["s", h, g, i][:],
+                scalar1=offs[h][:, i, g : g + 1],
+                scalar2=run_max[h][:, i, g - 1 : g] if g > 0 else None,
+                op0=ALU.add,
+                op1=ALU.max,
+                accum_out=run_max[h][:, i, g : g + 1],
+            )
+
+        def nb(h, i):
+            nc.scalar.activation(out=exp_bias[h][:, i : i + 1], in_=run_max[h][:, i, G - 1 : G], func=ACT.Copy, scale=-SOFTMAX_SCALE)
+
+        def ex(h, i):
+            nc.scalar.activation(
+                out=scores[h, i][:],
+                in_=scores[h, i][:],
+                func=ACT.Exp,
+                bias=exp_bias[h][:, i : i + 1],
+                scale=SOFTMAX_SCALE,
+                accum_out=row_sum[h][:, i : i + 1],
+            )
+
+        def rc(h, i):
+            nc.vector.reciprocal(out=row_inv[h][:, i : i + 1], in_=row_sum[h][:, i : i + 1])
+
+        def st(h, i, g0, g1):
+            ws = per_head("ws", [P, (g1 - g0) * W], BF16)
+            cols = slice(g0 * W, g1 * W)
+            nc.vector.scalar_tensor_tensor(
+                out=ws[:], in0=scores[h, i][:, cols], scalar=row_inv[h][:, i : i + 1], in1=vs_rows[h][:, cols], op0=ALU.mult, op1=ALU.mult
+            )
+            live["ws", h, i, g0] = ws
+
+        def tw(h, i, g0, g1):
+            ws = live["ws", h, i, g0]
+            turn(("w", h, i, g0), [words(ws[:, r * W : (r + 1) * W]) for r in range(g1 - g0)])
+
+        def cw(h, i, g0, g1):
+            live["wt", h, i, g0] = per_head("w_t", [P, (g1 - g0) * P, PACK], BF16)
+            turn_out(("w", h, i, g0), live["wt", h, i, g0][:], "s")
+
+        def qw(h, i, g0, g1):
+            quantize(("qw", h, i, g0), per_head, "w", live["wt", h, i, g0][:])
+
+        def out_parts(h, i):
+            if (h, i) == (H - 1, PACK - 1):
+                return [slice(0, D // 2), slice(D // 2, D)]
+            return [slice(0, D)]
+
+        def mo(h, i, g0, g1):
+            parts = out_parts(h, i)
+            for c, cols in enumerate(parts):
+                if g0 == 0 and h < H - 1:
+                    live["o", h, i, c] = out_pool.tile([P, D], F32, name="out_bank", tag="out_bank")
+                elif g0 == 0:
+                    live["o", h, i, c] = acc_pool.tile([P, D // len(parts)], F32, name="acc_bank", tag="acc_bank")
+                for g in range(g0, g1):
+                    mx(live["o", h, i, c][:], live["qw", h, i, g0], slice((g - g0) * P, (g - g0 + 1) * P), live["qv", h, g], cols,
+                       g == 0, g == G - 1)
+
+        def co(h, i, c):
+            cols = out_parts(h, i)[c]
+            nc.scalar.copy(out=result[h][:, i, cols], in_=live["o", h, i, c][:])
+            nc.sync.dma_start(out=out_0[h].rearrange("(p j) d -> p j d", j=PACK)[:, i, cols], in_=result[h][:, i, cols])
+
+        def io(h, c):
+            rounded = kept("rounded%d%d" % (h, c), [P, D // 2, PACK], BF16)
+            (nc.vector.tensor_copy if h == H - 1 else nc.scalar.copy)(
+                out=rounded[:].rearrange("p (c i) j -> p c j i", i=4),
+                in_=result[h][:, :, c * D // 2 : (c + 1) * D // 2].rearrange("p j (c i) -> p c j i", i=4),
+            )
+            live["r", h, c] = rounded
+
+        def qo(h, c):
+            if c == 0:
+                live["qo", h] = (kept("out_codes%d" % h, [P, D], U32), kept("out_scales%d" % h, [P, D], U8))
+            codes, scales = live["qo", h]
+            cols = slice(c * D // 2, (c + 1) * D // 2)
+            nc.vector.quantize_mx(
+                out=codes[:, cols].bitcast(FP8X4), scales=scales[:, cols], in_=live["r", h, c][:].rearrange("p c j -> p (c j)")
+            )
+            out_words = out_1[0].rearrange("p m t -> p (m t)").bitcast(I32)
+            nc.sync.dma_start(out=out_words[:, h * D + cols.start : h * D + cols.stop], in_=codes[:, cols].bitcast(I32))
+            if c == 1:
+                for quad in range(4):
+                    queue = nc.scalar if h == H - 1 and quad % 2 else nc.sync
+                    queue.dma_start(
+                        out=out_2[0, 4 * quad : 4 * quad + 4, h * D : (h + 1) * D].bitcast(I32),
+                        in_=scales[32 * quad : 32 * quad + 4, :].bitcast(I32),
+                    )
+
+        steps = {"tz": tz, "cz": cz, "tq": tq, "cq": cq, "tk": tk, "ck": ck, "off": off, "coff": coff, "mq": mq, "qq": qq, "qk": qk,
+                 "iv": iv, "qv": qv, "ms": ms, "sp": sp, "nb": nb, "ex": ex, "rc": rc, "st": st, "tw": tw, "cw": cw, "qw": qw,
+                 "mo": mo, "co": co, "io": io, "qo": qo}
+        for op in schedule():
+            steps[op[0]](*op[1:])

@@ -34,14 +34,18 @@ def engine_orders():
     def each(name, h, i):
         return [(name, h, i) + piece for piece in pieces(h, i)]
 
-    pe += [("tq", 0, 0), ("tz",), ("tq", 0, 1), ("tk", 0, 0, 0), ("tk", 0, 0, 1), ("tk", 0, 1, 0), ("off", 0), ("tk", 0, 1, 1)]
-    act += [("cq", 0, 1), ("ck", 0, 0, 0), ("ck", 0, 0, 1), ("ck", 0, 1, 0), ("coff", 0), ("ck", 0, 1, 1)]
-    dve += [("cq", 0, 0), ("cz",), ("mq", 0, 0), ("qk", 0, 0), ("qq", 0, 0)]
+    def weave(first, second):
+        return [step for pair in zip(first, second) for step in pair]
+
+    pe += [("warm", 0, 6), ("tq", 0, 0), ("tz",), ("tq", 0, 1), ("warm", 1, 2), ("tk", 0, 0, 0), ("tk", 0, 0, 1), ("warm", 2, 2), ("off", 0)]
+    pe += [("tk", 0, 1, 0)]
+    act += [("cq", 0, 1), ("ck", 0, 0, 0), ("ck", 0, 0, 1), ("coff", 0), ("ck", 0, 1, 0), ("iv", 0, 0, 0), ("ck", 0, 1, 1)]
+    dve += [("cq", 0, 0), ("cz",), ("mq", 0, 0, 0, 2), ("mq", 0, 0, 2, 4), ("mq", 0, 1, 0, 4), ("qq", 0, 0), ("qk", 0, 0), ("qq", 0, 1)]
     for h in range(H):
         first, last = h == 0, h == H - 1
         for g in range(G):
             if first and g == 0:
-                pe += [("ms", h, g, 0), ("ms", h, g, 1), ("ms", h, g, 2), ("tk", h, 2, 0), ("ms", h, g, 3), ("tk", h, 2, 1)]
+                pe += [("ms", h, g, 0), ("ms", h, g, 1), ("tk", 0, 1, 1), ("ms", h, g, 2), ("tk", h, 2, 0), ("ms", h, g, 3), ("tk", h, 2, 1)]
             elif g == 0:
                 pe += [("ms", h, g, 0), ("ms", h, g, 1), ("ms", h, g, 2), ("tk", h, 2, 0)] + each("mo", h - 1, 2)
                 pe += [("ms", h, g, 3), ("tk", h, 2, 1)] + each("mo", h - 1, 3)
@@ -52,9 +56,15 @@ def engine_orders():
             if not last and g == 2:
                 pe += [("tq", h + 1, b) for b in both] + [("tk", h + 1, 0, 0)]
             if not last and g == 3:
-                pe += [("tk", h + 1, 0, 1), ("off", h + 1)]
+                pe += [("tk", h + 1, 0, 1), ("bv", h, 0), ("off", h + 1), ("bv", h, 1)]
+            if last and g == 3:
+                pe += [("bv", h, b) for b in both]
             if g < G - 1:
-                dve += [("mq", h, g + 1), ("sp", h, g, 0), ("qq", h, g + 1), ("sp", h, g, 1)]
+                if first and g == 0:
+                    dve += [("sp", h, g, 0), ("sp", h, g, 1), ("sp", h, g, 2), ("qk", h, g + 1), ("sp", h, g, 3)]
+                    continue
+                else:
+                    dve += [("mq", h, g + 1, 0, 4), ("sp", h, g, 0), ("qq", h, g + 1), ("sp", h, g, 1)]
                 if not first and g == 0:
                     dve += each("qw", h - 1, 3)
                 dve += [("qk", h, g + 1), ("sp", h, g, 2)]
@@ -62,30 +72,30 @@ def engine_orders():
                     dve += [("qo", h - 1, c) for c in both]
                 dve += [("sp", h, g, 3)]
         if first:
-            act += [("iv", h, 0, b) for b in both] + [("ck", h, 2, b) for b in both] + [("iv", h, 1, b) for b in both]
+            act += [("iv", h, 0, 1)] + [("ck", h, 2, b) for b in both] + [("iv", h, 1, b) for b in both]
             act += [("ck", h, 3, b) for b in both] + [("iv", h, g, b) for g in (2, 3) for b in both]
         else:
             act += [("ck", h, 2, 0), ("iv", h, 0, 1), ("co", h - 1, 2, 0), ("ck", h, 2, 1), ("iv", h, 1, 0), ("co", h - 1, 3, 0), ("iv", h, 1, 1)]
             act += [("ck", h, 3, 0), ("ck", h, 3, 1), ("io", h - 1, 0), ("io", h - 1, 1)] + [("iv", h, g, b) for g in (2, 3) for b in both]
         dve += [("sp", h, 3, 0), ("qv", h, 0), ("sp", h, 3, 1), ("qv", h, 1), ("sp", h, 3, 2), ("sp", h, 3, 3), ("rc", h, 0), ("qv", h, 2)]
-        dve += each("st", h, 0) + [("rc", h, 1), ("qv", h, 3)] + each("st", h, 1) + [("rc", h, 2)] + each("qw", h, 0)
-        dve += each("st", h, 2) + [("rc", h, 3)]
-        pe += each("tw", h, 0) + each("tw", h, 1) + each("mo", h, 0) + each("tw", h, 2)
+        dve += each("st", h, 0) + [("rc", h, 1), ("qv", h, 3)] + each("st", h, 1) + [("rc", h, 2)]
+        dve += weave(each("qw", h, 0), each("st", h, 2)) + [("rc", h, 3)]
+        pe += each("tw", h, 0) + [("warm", 3 + 2 * h, 2 * h)] + each("tw", h, 1)[:1] + [("warm", 4 + 2 * h, 2 * h)] + each("tw", h, 1)[1:] + weave(each("mo", h, 0), each("tw", h, 2))
         if not last:
             act += [("cq", h + 1, 0), ("cq", h + 1, 1), ("nb", h, 0), ("ck", h + 1, 0, 0)]
             act += [("ex", h, 0), ("nb", h, 1), ("ck", h + 1, 0, 1), ("ex", h, 1), ("nb", h, 2), ("nb", h, 3), ("coff", h + 1), ("ex", h, 2)]
             act += each("cw", h, 0) + [("ex", h, 3)] + each("cw", h, 1) + [("co", h, 0, 0)] + each("cw", h, 2)
             act += [("ck", h + 1, 1, 0), ("ck", h + 1, 1, 1), ("co", h, 1, 0), ("iv", h + 1, 0, 0)] + each("cw", h, 3)
             tail = each("st", h, 3)
-            dve += [("mq", h + 1, 0)] + each("qw", h, 1) + [("qk", h + 1, 0), tail[0], ("qq", h + 1, 0), tail[1]] + each("qw", h, 2)
-            pe += [("tk", h + 1, 1, b) for b in both] + each("mo", h, 1) + each("tw", h, 3)
+            dve += [("mq", h + 1, 0, 0, 4)] + each("qw", h, 1)[:1] + [("qk", h + 1, 0), tail[0]] + each("qw", h, 1)[1:] + [("qq", h + 1, 0), tail[1]] + each("qw", h, 2)
+            pe += [("tk", h + 1, 1, b) for b in both] + weave(each("mo", h, 1), each("tw", h, 3))
         else:
             act += [("nb", h, 0), ("ex", h, 0), ("nb", h, 1), ("nb", h, 2), ("ex", h, 1), ("nb", h, 3), ("ex", h, 2)]
             act += each("cw", h, 0) + [("ex", h, 3)] + each("cw", h, 1) + [("co", h, 0, 0)] + each("cw", h, 2)
             act += each("cw", h, 3)[:1] + [("co", h, 1, 0)] + each("cw", h, 3)[1:] + [("co", h, 2, 0), ("co", h, 3, 0), ("co", h, 3, 1)]
-            dve += each("qw", h, 1) + each("st", h, 3)[:2] + each("qw", h, 2) + each("st", h, 3)[2:] + each("qw", h, 3)
+            dve += weave(each("qw", h, 1), each("st", h, 3)) + each("qw", h, 2)[:1] + each("st", h, 3)[2:] + each("qw", h, 2)[1:] + each("qw", h, 3)
             dve += [("io", h, 0), ("io", h, 1), ("qo", h, 0), ("qo", h, 1)]
-            pe += each("mo", h, 1) + each("tw", h, 3)[:2] + each("mo", h, 2)[:1] + each("tw", h, 3)[2:] + each("mo", h, 2)[1:] + each("mo", h, 3)
+            pe += weave(each("mo", h, 1), each("tw", h, 3)) + each("mo", h, 2)[:1] + each("tw", h, 3)[2:] + each("mo", h, 2)[1:] + each("mo", h, 3)
     return pe, act, dve
 
 
@@ -98,8 +108,9 @@ def producers(step):
         "ck": lambda h, g, b: [("tk", h, g, b)],
         "off": lambda h: [("cz",)] + [("cq", h, b) for b in both],
         "coff": lambda h: [("off", h)],
-        "mq": lambda h, g: [("cz",)] + [("cq", h, b) for b in both],
-        "qq": lambda h, g: [("mq", h, g)],
+        "mq": lambda h, g, i0, i1: [("cz",)] + [("cq", h, b) for b in range(i0 // 2, i1 // 2)],
+        "qq": lambda h, g: [("mq", h, g, 2 if (h, g) == (0, 0) else 0, 4)],
+        "bv": lambda h, b: [("cz",)],
         "qk": lambda h, g: [("ck", h, g, b) for b in both],
         "qv": lambda h, g: [("iv", h, g, b) for b in both],
         "ms": lambda h, g, i: [("qq", h, g), ("qk", h, g)],
@@ -107,7 +118,7 @@ def producers(step):
         "nb": lambda h, i: [("sp", h, G - 1, i)],
         "ex": lambda h, i: [("nb", h, i)],
         "rc": lambda h, i: [("ex", h, i)],
-        "st": lambda h, i, g0, g1: [("rc", h, i)],
+        "st": lambda h, i, g0, g1: [("rc", h, i), ("bv", h, g0 // 2)],
         "tw": lambda h, i, g0, g1: [("st", h, i, g0, g1)],
         "cw": lambda h, i, g0, g1: [("tw", h, i, g0, g1)],
         "qw": lambda h, i, g0, g1: [("cw", h, i, g0, g1)],
@@ -136,8 +147,7 @@ def tile_kivigroupedscalefoldedattention_x1_kernel(tc, q, k_code, k_scale, k_zer
     with ExitStack() as ctx:
         keep = ctx.enter_context(tc.tile_pool(name="keep", bufs=1))
         stage = ctx.enter_context(tc.tile_pool(name="stage", bufs=3))
-        acc_pool = ctx.enter_context(tc.psum_pool(name="acc", bufs=3))
-        out_pool = ctx.enter_context(tc.psum_pool(name="out", bufs=1))
+        banks = ctx.enter_context(tc.psum_pool(name="banks", bufs=1))
         turn_pool = ctx.enter_context(tc.psum_pool(name="turn", bufs=4))
         ctx.enter_context(tc.manual_schedule())
 
@@ -147,6 +157,9 @@ def tile_kivigroupedscalefoldedattention_x1_kernel(tc, q, k_code, k_scale, k_zer
         def staged(tag, shape, dtype):
             return stage.tile(shape, dtype, name=tag, tag=tag, align_bytes=64)
 
+        def bank_tile(number, shape, dtype):
+            return banks.tile(shape, dtype, name="bank%d" % number, tag="bank%d" % number)
+
         def per_head(tag, shape, dtype):
             return stage.tile(shape, dtype, name=tag, tag=tag, bufs=4, align_bytes=64)
 
@@ -154,10 +167,12 @@ def tile_kivigroupedscalefoldedattention_x1_kernel(tc, q, k_code, k_scale, k_zer
         nc.gpsimd.memset(factor_rows[:].bitcast(I32), 0)
         ident = kept("ident", [P, P], F32)
         make_identity(nc, ident[:])
+        pick = kept("pick", [P, H * G], BF16)
+        nc.gpsimd.tensor_copy(out=pick[:], in_=ident[:, 2 * H * G : 3 * H * G])
         warm = kept("warm", [P, 1], F32)
         nc.scalar.activation(out=warm[:], in_=ident[:, 0:1], func=ACT.Exp)
 
-        q_rows, k_rows, v_rows, vs_rows = {}, {}, {}, {}
+        q_rows, k_rows, v_rows = {}, {}, {}
 
         def load_q(h):
             src = q[h].rearrange("(p j) d -> p j d", j=PACK)
@@ -166,7 +181,7 @@ def tile_kivigroupedscalefoldedattention_x1_kernel(tc, q, k_code, k_scale, k_zer
                 nc.sync.dma_start(out=q_rows[h, b][:], in_=src[:, 2 * b : 2 * b + 2, :])
 
         def load_k(h, g):
-            src = k_code[h, g].rearrange("(r p) d -> p r d", p=P)
+            src = k_code[h, g].rearrange("(p j) d -> p j d", j=PACK)
             for b in range(2):
                 k_rows[h, g, b] = kept("k_rows%d%d%d" % (h, g, b), [P, 2, D], BF16)
                 nc.sync.dma_start(out=k_rows[h, g, b][:], in_=src[:, 2 * b : 2 * b + 2, :])
@@ -175,13 +190,10 @@ def tile_kivigroupedscalefoldedattention_x1_kernel(tc, q, k_code, k_scale, k_zer
             v_rows[h, g] = per_head("v_rows", [P, PACK, D], BF16)
             nc.sync.dma_start(out=v_rows[h, g][:], in_=v_code[h, g * W : (g + 1) * W, :].rearrange("(p j) d -> p j d", j=PACK))
 
-        def load_vs(h):
-            vs_rows[h] = kept("vs_rows%d" % h, [P, T], BF16)
-            nc.sync.dma_start(out=vs_rows[h][:], in_=v_scale[h].partition_broadcast(P))
-
         load_q(0)
         nc.sync.dma_start(out=factor_rows[0 : H * G, :], in_=k_scale.rearrange("h g d -> (h g) d"))
         nc.sync.dma_start(out=factor_rows[H * G : 2 * H * G, :], in_=k_zero.rearrange("h g d -> (h g) d"))
+        nc.sync.dma_start(out=factor_rows[2 * H * G : 3 * H * G, :], in_=v_scale.rearrange("h (g t) -> (h g) t", g=G))
         load_k(0, 0)
         for h in range(H):
             load_k(h, 1)
@@ -194,7 +206,6 @@ def tile_kivigroupedscalefoldedattention_x1_kernel(tc, q, k_code, k_scale, k_zer
             if h + 1 < H:
                 load_q(h + 1)
                 load_k(h + 1, 0)
-            load_vs(h)
 
         factors = kept("factors", [P, 2 * H * G, PACK], BF16)
         q_t = {h: kept("q_t%d" % h, [P, N, PACK], BF16) for h in range(H)}
@@ -210,11 +221,11 @@ def tile_kivigroupedscalefoldedattention_x1_kernel(tc, q, k_code, k_scale, k_zer
         def words(tile_ap):
             return tile_ap.bitcast(F32)
 
-        def turn(key, sources):
+        def turn(key, sources, step=2):
             bank = turn_pool.tile([P, len(sources), 2, P], F32, name="turn_bank", tag="turn_bank")
             for r, src in enumerate(sources):
                 for u in range(2):
-                    nc.tensor.transpose(bank[:, r, u, :], src[:, u : 2 * P : 2], ident[:])
+                    nc.tensor.transpose(bank[:, r, u, :], src[:, u : 2 * P : 2] if step == 2 else src[:, u * P : (u + 1) * P], ident[:])
             live[key] = bank
 
         def turn_out(key, dst, engine):
@@ -242,8 +253,17 @@ def tile_kivigroupedscalefoldedattention_x1_kernel(tc, q, k_code, k_scale, k_zer
                 stop=stop,
             )
 
+        zeros = kept("zeros", [P, W], BF16)
+        nc.vector.memset(zeros[:].bitcast(I32), 0)
+
+        def warm_pass(n, count):
+            if count:
+                idle_bank = bank_tile(2 if n < 3 else 3, [P, W], F32)
+            for repeat in range(count):
+                nc.tensor.matmul(idle_bank[:], lhsT=zeros[:, 0:P], rhs=zeros[:], start=True, stop=True)
+
         def tz():
-            bank = out_pool.tile([P, 2, P], F32, name="out_bank", tag="out_bank")
+            bank = bank_tile(3, [P, 2, P], F32)
             for u in range(2):
                 nc.tensor.transpose(bank[:, u, :], words(factor_rows[:])[:, u : 2 * P : 2], ident[:])
             live["z"] = bank
@@ -266,10 +286,11 @@ def tile_kivigroupedscalefoldedattention_x1_kernel(tc, q, k_code, k_scale, k_zer
         def ck(h, g, b):
             if b == 0:
                 live["kt", h, g] = staged("k_t", [P, W, PACK], BF16)
-            turn_out(("k", h, g, b), live["kt", h, g][:, 2 * P * b : 2 * P * (b + 1), :], "s")
+            dst = live["kt", h, g][:, 2 * P * b : 2 * P * (b + 1), :].rearrange("p c j -> p (c j)").bitcast(F32)
+            nc.scalar.copy(out=dst.rearrange("p (m e u) -> p m e u", e=2, u=2), in_=live["k", h, g, b][:].rearrange("p e u m -> p m e u"))
 
         def off(h):
-            bank = out_pool.tile([P, PACK, G], F32, name="out_bank", tag="out_bank")
+            bank = bank_tile(3, [P, PACK, G], F32)
             first = H * G + h * G
             for i in range(PACK):
                 for j in range(PACK):
@@ -285,12 +306,12 @@ def tile_kivigroupedscalefoldedattention_x1_kernel(tc, q, k_code, k_scale, k_zer
         def coff(h):
             nc.scalar.copy(out=offs[h][:], in_=live["off", h][:])
 
-        def mq(h, g):
-            qs = staged("qs", [P, N, PACK], BF16)
-            nc.vector.tensor_tensor(
-                out=qs[:], in0=q_t[h][:], in1=factors[:, h * G + g : h * G + g + 1, :].to_broadcast([P, N, PACK]), op=ALU.mult
-            )
-            live["qs", h, g] = qs
+        def mq(h, g, i0, i1):
+            if i0 == 0:
+                live["qs", h, g] = staged("qs", [P, N, PACK], BF16)
+            rows = slice(i0 * P, i1 * P)
+            factor = factors[:, h * G + g : h * G + g + 1, :].to_broadcast([P, (i1 - i0) * P, PACK])
+            nc.vector.tensor_tensor(out=live["qs", h, g][:, rows, :], in0=q_t[h][:, rows, :], in1=factor, op=ALU.mult)
 
         def qq(h, g):
             quantize(("qq", h, g), staged, "qs", live["qs", h, g][:])
@@ -311,7 +332,7 @@ def tile_kivigroupedscalefoldedattention_x1_kernel(tc, q, k_code, k_scale, k_zer
             quantize(("qv", h, g), per_head, "v", live["vt", h, g][:])
 
         def ms(h, g, i):
-            bank = acc_pool.tile([P, W], F32, name="acc_bank", tag="acc_bank")
+            bank = bank_tile((g * PACK + i) % 3, [P, W], F32)
             mx(bank[:], live["qq", h, g], slice(i * P, (i + 1) * P), live["qk", h, g], slice(0, W), True, True)
             live["s", h, g, i] = bank
 
@@ -344,17 +365,31 @@ def tile_kivigroupedscalefoldedattention_x1_kernel(tc, q, k_code, k_scale, k_zer
         def rc(h, i):
             nc.vector.reciprocal(out=row_inv[h][:, i : i + 1], in_=row_sum[h][:, i : i + 1])
 
+        def bv(h, b):
+            bank = bank_tile(1 + b, [P, 2, W], BF16)
+            for r in range(2):
+                row = h * G + 2 * b + r
+                nc.tensor.matmul(
+                    bank[:, r, :],
+                    lhsT=pick[:, row : row + 1].to_broadcast([P, P]),
+                    rhs=factor_rows[:].rearrange("p (m u e) -> p u m e", u=2, e=2),
+                    start=True,
+                    stop=True,
+                )
+            live["vs", h, b] = bank
+
         def st(h, i, g0, g1):
             ws = per_head("ws", [P, (g1 - g0) * W], BF16)
             cols = slice(g0 * W, g1 * W)
+            vs = live["vs", h, g0 // 2][:, g0 % 2 : g0 % 2 + g1 - g0, :].rearrange("p r t -> p (r t)")
             nc.vector.scalar_tensor_tensor(
-                out=ws[:], in0=scores[h, i][:, cols], scalar=row_inv[h][:, i : i + 1], in1=vs_rows[h][:, cols], op0=ALU.mult, op1=ALU.mult
+                out=ws[:], in0=scores[h, i][:, cols], scalar=row_inv[h][:, i : i + 1], in1=vs, op0=ALU.mult, op1=ALU.mult
             )
             live["ws", h, i, g0] = ws
 
         def tw(h, i, g0, g1):
             ws = live["ws", h, i, g0]
-            turn(("w", h, i, g0), [words(ws[:, r * W : (r + 1) * W]) for r in range(g1 - g0)])
+            turn(("w", h, i, g0), [words(ws[:, r * W : (r + 1) * W]) for r in range(g1 - g0)], step=1)
 
         def cw(h, i, g0, g1):
             live["wt", h, i, g0] = per_head("w_t", [P, (g1 - g0) * P, PACK], BF16)
@@ -371,10 +406,8 @@ def tile_kivigroupedscalefoldedattention_x1_kernel(tc, q, k_code, k_scale, k_zer
         def mo(h, i, g0, g1):
             parts = out_parts(h, i)
             for c, cols in enumerate(parts):
-                if g0 == 0 and h < H - 1:
-                    live["o", h, i, c] = out_pool.tile([P, D], F32, name="out_bank", tag="out_bank")
-                elif g0 == 0:
-                    live["o", h, i, c] = acc_pool.tile([P, D // len(parts)], F32, name="acc_bank", tag="acc_bank")
+                if g0 == 0:
+                    live["o", h, i, c] = bank_tile(c if h == H - 1 and i % 2 else 3, [P, D // len(parts)], F32)
                 for g in range(g0, g1):
                     mx(live["o", h, i, c][:], live["qw", h, i, g0], slice((g - g0) * P, (g - g0 + 1) * P), live["qv", h, g], cols,
                        g == 0, g == G - 1)
@@ -410,7 +443,7 @@ def tile_kivigroupedscalefoldedattention_x1_kernel(tc, q, k_code, k_scale, k_zer
                         in_=scales[32 * quad : 32 * quad + 4, :].bitcast(I32),
                     )
 
-        steps = {"tz": tz, "cz": cz, "tq": tq, "cq": cq, "tk": tk, "ck": ck, "off": off, "coff": coff, "mq": mq, "qq": qq, "qk": qk,
+        steps = {"tz": tz, "cz": cz, "tq": tq, "cq": cq, "tk": tk, "ck": ck, "off": off, "coff": coff, "mq": mq, "warm": warm_pass, "bv": bv, "qq": qq, "qk": qk,
                  "iv": iv, "qv": qv, "ms": ms, "sp": sp, "nb": nb, "ex": ex, "rc": rc, "st": st, "tw": tw, "cw": cw, "qw": qw,
                  "mo": mo, "co": co, "io": io, "qo": qo}
         for op in schedule():

@@ -27,6 +27,10 @@ def pieces(h, i):
     return [(0, 2), (2, 4)]
 
 
+def q_parts(h):
+    return [(i, i + 1) for i in range(PACK)] if h == 0 else [(0, 2), (2, 4)]
+
+
 def engine_orders():
     pe, act, dve = [], [], []
     both = (0, 1)
@@ -37,10 +41,12 @@ def engine_orders():
     def weave(first, second):
         return [step for pair in zip(first, second) for step in pair]
 
-    pe += [("warm", 0, 6), ("tq", 0, 0), ("tz",), ("tq", 0, 1), ("warm", 1, 2), ("tk", 0, 0, 0), ("tk", 0, 0, 1), ("warm", 2, 2), ("off", 0)]
+    pe += [("warm", 0, 5), ("tz",)] + [("tq", 0, i, i + 1) for i in range(PACK)]
+    pe += [("warm", 1, 2), ("tk", 0, 0, 0), ("tk", 0, 0, 1), ("warm", 2, 2), ("off", 0)]
     pe += [("tk", 0, 1, 0)]
-    act += [("cq", 0, 1), ("ck", 0, 0, 0), ("ck", 0, 0, 1), ("coff", 0), ("ck", 0, 1, 0), ("iv", 0, 0, 0), ("ck", 0, 1, 1)]
-    dve += [("cq", 0, 0), ("cz",), ("mq", 0, 0, 0, 2), ("mq", 0, 0, 2, 4), ("mq", 0, 1, 0, 4), ("qq", 0, 0), ("qk", 0, 0), ("qq", 0, 1)]
+    act += [("cq", 0, i, i + 1) for i in range(PACK)] + [("ck", 0, 0, 0), ("ck", 0, 0, 1), ("coff", 0), ("ck", 0, 1, 0), ("iv", 0, 0, 0), ("ck", 0, 1, 1)]
+    dve += [("cz",)] + [("mq", 0, 0, i, i + 1) for i in range(PACK)]
+    dve += [("mq", 0, 1, 0, 4), ("qq", 0, 0), ("qq", 0, 1), ("qk", 0, 0), ("mq", 0, 2, 0, 4)]
     for h in range(H):
         first, last = h == 0, h == H - 1
         for g in range(G):
@@ -48,54 +54,55 @@ def engine_orders():
                 pe += [("ms", h, g, 0), ("ms", h, g, 1), ("tk", 0, 1, 1), ("ms", h, g, 2), ("tk", h, 2, 0), ("ms", h, g, 3), ("tk", h, 2, 1)]
             elif g == 0:
                 pe += [("ms", h, g, 0), ("ms", h, g, 1), ("ms", h, g, 2), ("tk", h, 2, 0)] + each("mo", h - 1, 2)
-                pe += [("ms", h, g, 3), ("tk", h, 2, 1)] + each("mo", h - 1, 3)
+                pe += [("ms", h, g, 3), ("tk", h, 2, 1)]
+            elif g == 1 and not first:
+                pe += [("ms", h, g, 0), ("ms", h, g, 1), ("ms", h, g, 2)] + each("mo", h - 1, 3) + [("ms", h, g, 3), ("tk", h, 3, 0), ("tk", h, 3, 1)]
             elif g == 1:
                 pe += [("ms", h, g, 0), ("ms", h, g, 1), ("ms", h, g, 2), ("tk", h, 3, 0), ("ms", h, g, 3), ("tk", h, 3, 1)]
             else:
                 pe += [("ms", h, g, i) for i in range(PACK)]
             if not last and g == 2:
-                pe += [("tq", h + 1, b) for b in both] + [("tk", h + 1, 0, 0)]
-            if not last and g == 3:
-                pe += [("tk", h + 1, 0, 1), ("bv", h, 0), ("off", h + 1), ("bv", h, 1)]
-            if last and g == 3:
+                pe += [("tq", h + 1, 0, 2), ("tq", h + 1, 2, 4)]
+            if g == 3:
                 pe += [("bv", h, b) for b in both]
             if g < G - 1:
                 if first and g == 0:
                     dve += [("sp", h, g, 0), ("sp", h, g, 1), ("sp", h, g, 2), ("qk", h, g + 1), ("sp", h, g, 3)]
                     continue
+                elif first:
+                    dve += [("mq", h, g + 2, 0, 4)] * (g == 1) + [("sp", h, g, 0), ("qq", h, g + 1), ("sp", h, g, 1)]
                 else:
                     dve += [("mq", h, g + 1, 0, 4), ("sp", h, g, 0), ("qq", h, g + 1), ("sp", h, g, 1)]
                 if not first and g == 0:
                     dve += each("qw", h - 1, 3)
                 dve += [("qk", h, g + 1), ("sp", h, g, 2)]
-                if not first and g == 2:
-                    dve += [("qo", h - 1, c) for c in both]
                 dve += [("sp", h, g, 3)]
         if first:
             act += [("iv", h, 0, 1)] + [("ck", h, 2, b) for b in both] + [("iv", h, 1, b) for b in both]
             act += [("ck", h, 3, b) for b in both] + [("iv", h, g, b) for g in (2, 3) for b in both]
         else:
-            act += [("ck", h, 2, 0), ("iv", h, 0, 1), ("co", h - 1, 2, 0), ("ck", h, 2, 1), ("iv", h, 1, 0), ("co", h - 1, 3, 0), ("iv", h, 1, 1)]
-            act += [("ck", h, 3, 0), ("ck", h, 3, 1), ("io", h - 1, 0), ("io", h - 1, 1)] + [("iv", h, g, b) for g in (2, 3) for b in both]
+            act += [("ck", h, 2, 0), ("iv", h, 0, 1), ("co", h - 1, 2, 0), ("ck", h, 2, 1), ("iv", h, 1, 0), ("iv", h, 1, 1), ("co", h - 1, 3, 0)]
+            act += [("iv", h, 2, 0), ("ck", h, 3, 0), ("ck", h, 3, 1), ("iv", h, 2, 1), ("iv", h, 3, 0), ("iv", h, 3, 1)]
         dve += [("sp", h, 3, 0), ("qv", h, 0), ("sp", h, 3, 1), ("qv", h, 1), ("sp", h, 3, 2), ("sp", h, 3, 3), ("rc", h, 0), ("qv", h, 2)]
         dve += each("st", h, 0) + [("rc", h, 1), ("qv", h, 3)] + each("st", h, 1) + [("rc", h, 2)]
         dve += weave(each("qw", h, 0), each("st", h, 2)) + [("rc", h, 3)]
-        pe += each("tw", h, 0) + [("warm", 3 + 2 * h, 2 * h)] + each("tw", h, 1)[:1] + [("warm", 4 + 2 * h, 2 * h)] + each("tw", h, 1)[1:] + weave(each("mo", h, 0), each("tw", h, 2))
+        pe += each("tw", h, 0) + [("off", h + 1)] * (not last) + [("warm", 3 + 2 * h, 2 * h)] + each("tw", h, 1)[:1] + [("warm", 4 + 2 * h, 2 * h)] + each("tw", h, 1)[1:] + weave(each("mo", h, 0), each("tw", h, 2))
         if not last:
-            act += [("cq", h + 1, 0), ("cq", h + 1, 1), ("nb", h, 0), ("ck", h + 1, 0, 0)]
-            act += [("ex", h, 0), ("nb", h, 1), ("ck", h + 1, 0, 1), ("ex", h, 1), ("nb", h, 2), ("nb", h, 3), ("coff", h + 1), ("ex", h, 2)]
-            act += each("cw", h, 0) + [("ex", h, 3)] + each("cw", h, 1) + [("co", h, 0, 0)] + each("cw", h, 2)
-            act += [("ck", h + 1, 1, 0), ("ck", h + 1, 1, 1), ("co", h, 1, 0), ("iv", h + 1, 0, 0)] + each("cw", h, 3)
+            act += [("nb", h, 0), ("cq", h + 1, 0, 2), ("ex", h, 0), ("nb", h, 1), ("cq", h + 1, 2, 4), ("ex", h, 1), ("nb", h, 2), ("nb", h, 3)]
+            act += [("ex", h, 2)] + each("cw", h, 0) + [("coff", h + 1), ("ex", h, 3)] + each("cw", h, 1) + [("co", h, 0, 0)]
+            act += [("ck", h + 1, 0, 0), ("ck", h + 1, 0, 1)] + each("cw", h, 2)
+            act += [("co", h, 1, 0), ("ck", h + 1, 1, 0), ("ck", h + 1, 1, 1)] + each("cw", h, 3) + [("iv", h + 1, 0, 0)]
             tail = each("st", h, 3)
-            dve += [("mq", h + 1, 0, 0, 4)] + each("qw", h, 1)[:1] + [("qk", h + 1, 0), tail[0]] + each("qw", h, 1)[1:] + [("qq", h + 1, 0), tail[1]] + each("qw", h, 2)
-            pe += [("tk", h + 1, 1, b) for b in both] + weave(each("mo", h, 1), each("tw", h, 3))
+            dve += [("mq", h + 1, 0, 0, 4)] + each("qw", h, 1)[:1] + [tail[0]] + each("qw", h, 1)[1:] + [("qq", h + 1, 0), ("qk", h + 1, 0), tail[1]] + each("qw", h, 2)
+            pe += [("tk", h + 1, 0, b) for b in both] + each("mo", h, 1) + [("tk", h + 1, 1, b) for b in both] + each("tw", h, 3)
         else:
             act += [("nb", h, 0), ("ex", h, 0), ("nb", h, 1), ("nb", h, 2), ("ex", h, 1), ("nb", h, 3), ("ex", h, 2)]
             act += each("cw", h, 0) + [("ex", h, 3)] + each("cw", h, 1) + [("co", h, 0, 0)] + each("cw", h, 2)
             act += each("cw", h, 3)[:1] + [("co", h, 1, 0)] + each("cw", h, 3)[1:] + [("co", h, 2, 0), ("co", h, 3, 0), ("co", h, 3, 1)]
-            dve += weave(each("qw", h, 1), each("st", h, 3)) + each("qw", h, 2)[:1] + each("st", h, 3)[2:] + each("qw", h, 2)[1:] + each("qw", h, 3)
+            dve += each("qw", h, 1) + each("st", h, 3)[:1] + each("qw", h, 2) + each("st", h, 3)[1:] + each("qw", h, 3)[:1]
+            dve += [("io", h - 1, 0)] + each("qw", h, 3)[1:] + [("io", h - 1, 1), ("qo", h - 1, 0), ("qo", h - 1, 1)]
             dve += [("io", h, 0), ("io", h, 1), ("qo", h, 0), ("qo", h, 1)]
-            pe += weave(each("mo", h, 1), each("tw", h, 3)) + each("mo", h, 2)[:1] + each("tw", h, 3)[2:] + each("mo", h, 2)[1:] + each("mo", h, 3)
+            pe += each("mo", h, 1) + each("tw", h, 3)[:1] + each("mo", h, 2) + each("tw", h, 3)[1:] + each("mo", h, 3)
     return pe, act, dve
 
 
@@ -104,12 +111,12 @@ def producers(step):
     both = (0, 1)
     table = {
         "cz": lambda: [("tz",)],
-        "cq": lambda h, b: [("tq", h, b)],
+        "cq": lambda h, i0, i1: [("tq", h, i0, i1)],
         "ck": lambda h, g, b: [("tk", h, g, b)],
-        "off": lambda h: [("cz",)] + [("cq", h, b) for b in both],
+        "off": lambda h: [("cz",)] + [("cq", h) + part for part in q_parts(h)],
         "coff": lambda h: [("off", h)],
-        "mq": lambda h, g, i0, i1: [("cz",)] + [("cq", h, b) for b in range(i0 // 2, i1 // 2)],
-        "qq": lambda h, g: [("mq", h, g, 2 if (h, g) == (0, 0) else 0, 4)],
+        "mq": lambda h, g, i0, i1: [("cz",)] + [("cq", h) + part for part in q_parts(h) if i0 <= part[0] < i1],
+        "qq": lambda h, g: [("mq", h, g, 3 if (h, g) == (0, 0) else 0, 4)],
         "bv": lambda h, b: [("cz",)],
         "qk": lambda h, g: [("ck", h, g, b) for b in both],
         "qv": lambda h, g: [("iv", h, g, b) for b in both],
@@ -165,6 +172,9 @@ def tile_kivigroupedscalefoldedattention_x1_kernel(tc, q, k_code, k_scale, k_zer
 
         factor_rows = kept("factor_rows", [P, D], BF16)
         nc.gpsimd.memset(factor_rows[:].bitcast(I32), 0)
+        nc.scalar.dma_start(out=factor_rows[0 : H * G, :], in_=k_scale.rearrange("h g d -> (h g) d"))
+        nc.scalar.dma_start(out=factor_rows[H * G : 2 * H * G, :], in_=k_zero.rearrange("h g d -> (h g) d"))
+        nc.scalar.dma_start(out=factor_rows[2 * H * G : 3 * H * G, :], in_=v_scale.rearrange("h (g t) -> (h g) t", g=G))
         ident = kept("ident", [P, P], F32)
         make_identity(nc, ident[:])
         pick = kept("pick", [P, H * G], BF16)
@@ -176,9 +186,9 @@ def tile_kivigroupedscalefoldedattention_x1_kernel(tc, q, k_code, k_scale, k_zer
 
         def load_q(h):
             src = q[h].rearrange("(p j) d -> p j d", j=PACK)
-            for b in range(2):
-                q_rows[h, b] = kept("q_rows%d%d" % (h, b), [P, 2, D], BF16)
-                nc.sync.dma_start(out=q_rows[h, b][:], in_=src[:, 2 * b : 2 * b + 2, :])
+            for i0, i1 in q_parts(h):
+                q_rows[h, i0] = kept("q_rows%d%d" % (h, i0), [P, i1 - i0, D], BF16)
+                nc.sync.dma_start(out=q_rows[h, i0][:], in_=src[:, i0:i1, :])
 
         def load_k(h, g):
             src = k_code[h, g].rearrange("(p j) d -> p j d", j=PACK)
@@ -191,9 +201,6 @@ def tile_kivigroupedscalefoldedattention_x1_kernel(tc, q, k_code, k_scale, k_zer
             nc.sync.dma_start(out=v_rows[h, g][:], in_=v_code[h, g * W : (g + 1) * W, :].rearrange("(p j) d -> p j d", j=PACK))
 
         load_q(0)
-        nc.sync.dma_start(out=factor_rows[0 : H * G, :], in_=k_scale.rearrange("h g d -> (h g) d"))
-        nc.sync.dma_start(out=factor_rows[H * G : 2 * H * G, :], in_=k_zero.rearrange("h g d -> (h g) d"))
-        nc.sync.dma_start(out=factor_rows[2 * H * G : 3 * H * G, :], in_=v_scale.rearrange("h (g t) -> (h g) t", g=G))
         load_k(0, 0)
         for h in range(H):
             load_k(h, 1)
@@ -274,11 +281,11 @@ def tile_kivigroupedscalefoldedattention_x1_kernel(tc, q, k_code, k_scale, k_zer
                 in_=live["z"][:, :, 0 : 2 * H * G].rearrange("p u r -> p r u"),
             )
 
-        def tq(h, b):
-            turn(("q", h, b), [words(q_rows[h, b][:, r, :]) for r in range(2)])
+        def tq(h, i0, i1):
+            turn(("q", h, i0), [words(q_rows[h, i0][:, r, :]) for r in range(i1 - i0)])
 
-        def cq(h, b):
-            turn_out(("q", h, b), q_t[h][:, 2 * P * b : 2 * P * (b + 1), :], "v" if (h, b) == (0, 0) else "s")
+        def cq(h, i0, i1):
+            turn_out(("q", h, i0), q_t[h][:, P * i0 : P * i1, :], "s")
 
         def tk(h, g, b):
             turn(("k", h, g, b), [words(k_rows[h, g, b][:, r, :]) for r in range(2)])
@@ -413,34 +420,36 @@ def tile_kivigroupedscalefoldedattention_x1_kernel(tc, q, k_code, k_scale, k_zer
                        g == 0, g == G - 1)
 
         def co(h, i, c):
-            cols = out_parts(h, i)[c]
-            nc.scalar.copy(out=result[h][:, i, cols], in_=live["o", h, i, c][:])
-            nc.sync.dma_start(out=out_0[h].rearrange("(p j) d -> p j d", j=PACK)[:, i, cols], in_=result[h][:, i, cols])
+            parts = out_parts(h, i)
+            nc.scalar.copy(out=result[h][:, i, parts[c]], in_=live["o", h, i, c][:])
+            if c == len(parts) - 1:
+                nc.sync.dma_start(out=out_0[h].rearrange("(p j) d -> p j d", j=PACK)[:, i, :], in_=result[h][:, i, :])
 
         def io(h, c):
             rounded = kept("rounded%d%d" % (h, c), [P, D // 2, PACK], BF16)
-            (nc.vector.tensor_copy if h == H - 1 else nc.scalar.copy)(
+            nc.vector.tensor_copy(
                 out=rounded[:].rearrange("p (c i) j -> p c j i", i=4),
                 in_=result[h][:, :, c * D // 2 : (c + 1) * D // 2].rearrange("p j (c i) -> p c j i", i=4),
             )
             live["r", h, c] = rounded
 
+        out_codes = kept("out_codes", [P, H * D], U32)
+        out_scales = kept("out_scales", [P, H * D], U8)
+
         def qo(h, c):
-            if c == 0:
-                live["qo", h] = (kept("out_codes%d" % h, [P, D], U32), kept("out_scales%d" % h, [P, D], U8))
-            codes, scales = live["qo", h]
-            cols = slice(c * D // 2, (c + 1) * D // 2)
+            cols = slice(h * D + c * D // 2, h * D + (c + 1) * D // 2)
             nc.vector.quantize_mx(
-                out=codes[:, cols].bitcast(FP8X4), scales=scales[:, cols], in_=live["r", h, c][:].rearrange("p c j -> p (c j)")
+                out=out_codes[:, cols].bitcast(FP8X4), scales=out_scales[:, cols], in_=live["r", h, c][:].rearrange("p c j -> p (c j)")
             )
-            out_words = out_1[0].rearrange("p m t -> p (m t)").bitcast(I32)
-            nc.sync.dma_start(out=out_words[:, h * D + cols.start : h * D + cols.stop], in_=codes[:, cols].bitcast(I32))
             if c == 1:
+                head = slice(h * D, (h + 1) * D)
+                out_words = out_1[0].rearrange("p m t -> p (m t)").bitcast(I32)
+                nc.sync.dma_start(out=out_words[:, head], in_=out_codes[:, head].bitcast(I32))
+            if c == 1 and h == H - 1:
                 for quad in range(4):
-                    queue = nc.scalar if h == H - 1 and quad % 2 else nc.sync
-                    queue.dma_start(
-                        out=out_2[0, 4 * quad : 4 * quad + 4, h * D : (h + 1) * D].bitcast(I32),
-                        in_=scales[32 * quad : 32 * quad + 4, :].bitcast(I32),
+                    (nc.scalar if quad % 2 else nc.sync).dma_start(
+                        out=out_2[0, 4 * quad : 4 * quad + 4, :].bitcast(I32),
+                        in_=out_scales[32 * quad : 32 * quad + 4, :].bitcast(I32),
                     )
 
         steps = {"tz": tz, "cz": cz, "tq": tq, "cq": cq, "tk": tk, "ck": ck, "off": off, "coff": coff, "mq": mq, "warm": warm_pass, "bv": bv, "qq": qq, "qk": qk,

@@ -17,122 +17,148 @@ ACT = mybir.ActivationFunctionType
 
 P = 128
 PACK = 4
-W = 512
-SOFTMAX_SCALE = D ** -0.5
+W = T // G
+SOFTMAX_SCALE = D**-0.5
+HALVES = (0, 1)
+LAST_TILE = (H - 1, PACK - 1)
 
-
-def pieces(h, i):
-    if (h, i) == (H - 1, PACK - 1):
-        return [(0, 2), (2, 3), (3, 4)]
-    return [(0, 2), (2, 4)]
+TRANSPOSE_BANKS = 4
+SCORE_BANKS = 3
+V_SCALE_BANK = 1
+RESULT_BANK = 3
 
 
 def q_parts(h):
     return [(i, i + 1) for i in range(PACK)] if h == 0 else [(0, 2), (2, 4)]
 
 
+def weight_parts(h, i):
+    return [(0, 2), (2, 3), (3, 4)] if (h, i) == LAST_TILE else [(0, 2), (2, 4)]
+
+
+def product_parts(h, i):
+    return weight_parts(h, i) if i < 2 or (h, i) == LAST_TILE else [(0, G)]
+
+
+def value_parts():
+    return [(0, 2), (2, 3), (3, 4)]
+
+
+def channel_parts(split):
+    return [slice(c * D // 2, (c + 1) * D // 2) for c in HALVES] if split else [slice(0, D)]
+
+
 def engine_orders():
     pe, act, dve = [], [], []
-    both = (0, 1)
 
-    def each(name, h, i):
-        return [(name, h, i) + piece for piece in pieces(h, i)]
+    def both(name, h, g):
+        return [(name, h, g, b) for b in HALVES]
+
+    def parts(name, h, i):
+        split = product_parts if name in ("quantize_w", "multiply_v") else weight_parts
+        return [(name, h, i) + part for part in split(h, i)]
+
+    def tiles(name, h, g, first, end):
+        return [(name, h, g, i) for i in range(first, end)]
 
     def weave(first, second):
         return [step for pair in zip(first, second) for step in pair]
 
-    pe += [("warm", 0, 5), ("tz",)] + [("tq", 0, i, i + 1) for i in range(PACK)]
-    pe += [("warm", 1, 2), ("tk", 0, 0, 0), ("tk", 0, 0, 1), ("warm", 2, 2), ("off", 0)]
-    pe += [("tk", 0, 1, 0)]
-    act += [("cq", 0, i, i + 1) for i in range(PACK)] + [("ck", 0, 0, 0), ("ck", 0, 0, 1), ("coff", 0), ("ck", 0, 1, 0), ("iv", 0, 0, 0), ("ck", 0, 1, 1)]
-    dve += [("cz",)] + [("mq", 0, 0, i, i + 1) for i in range(PACK)]
-    dve += [("mq", 0, 1, 0, 4), ("qq", 0, 0), ("qq", 0, 1), ("qk", 0, 0), ("mq", 0, 2, 0, 4)]
+    first_q = [("turn_q", 0) + part for part in q_parts(0)]
+    pe += [("warm", 0, 3), first_q[0], ("turn_factors",)] + first_q[1:]
+    pe += [("warm", 1, 2)] + both("turn_k", 0, 0) + [("warm", 2, 2), ("offsets", 0)] + both("turn_k", 0, 1)
+    act += [("copy_q", 0) + part for part in q_parts(0)] + both("copy_k", 0, 0)
+    act += [("interleave_v", 0, 0, 0), ("copy_offsets", 0)] + both("copy_k", 0, 1)
+    dve += [("copy_factors",)] + [("scale_q", 0, 0) + part for part in q_parts(0)]
+    dve += [("scale_q", 0, 1, 0, PACK), ("scale_q", 0, 2, 0, PACK), ("quantize_qk", 0, 0), ("scale_q", 0, 3, 0, PACK)]
+
     for h in range(H):
         first, last = h == 0, h == H - 1
-        for g in range(G):
-            if first and g == 0:
-                pe += [("ms", h, g, 0), ("ms", h, g, 1), ("tk", 0, 1, 1), ("ms", h, g, 2), ("tk", h, 2, 0), ("ms", h, g, 3), ("tk", h, 2, 1)]
-            elif g == 0:
-                pe += [("ms", h, g, 0), ("ms", h, g, 1), ("ms", h, g, 2), ("tk", h, 2, 0)] + each("mo", h - 1, 2)
-                pe += [("ms", h, g, 3), ("tk", h, 2, 1)]
-            elif g == 1 and not first:
-                pe += [("ms", h, g, 0), ("ms", h, g, 1), ("ms", h, g, 2)] + each("mo", h - 1, 3) + [("ms", h, g, 3), ("tk", h, 3, 0), ("tk", h, 3, 1)]
-            elif g == 1:
-                pe += [("ms", h, g, 0), ("ms", h, g, 1), ("ms", h, g, 2), ("tk", h, 3, 0), ("ms", h, g, 3), ("tk", h, 3, 1)]
-            else:
-                pe += [("ms", h, g, i) for i in range(PACK)]
-            if not last and g == 2:
-                pe += [("tq", h + 1, 0, 2), ("tq", h + 1, 2, 4)]
-            if g == 3:
-                pe += [("bv", h, b) for b in both]
-            if g < G - 1:
-                if first and g == 0:
-                    dve += [("sp", h, g, 0), ("sp", h, g, 1), ("sp", h, g, 2), ("qk", h, g + 1), ("sp", h, g, 3)]
-                    continue
-                elif first:
-                    dve += [("mq", h, g + 2, 0, 4)] * (g == 1) + [("sp", h, g, 0), ("qq", h, g + 1), ("sp", h, g, 1)]
-                else:
-                    dve += [("mq", h, g + 1, 0, 4), ("sp", h, g, 0), ("qq", h, g + 1), ("sp", h, g, 1)]
-                if not first and g == 0:
-                    dve += each("qw", h - 1, 3)
-                dve += [("qk", h, g + 1), ("sp", h, g, 2)]
-                dve += [("sp", h, g, 3)]
+
+        for g in range(G - 1):
+            if not first:
+                dve += [("scale_q", h, g + 1, 0, PACK)]
+            dve += tiles("take_scores", h, g, 0, 2)
+            if not first and g == 0:
+                dve += parts("quantize_w", h - 1, 3)
+            dve += [("quantize_qk", h, g + 1)] + tiles("take_scores", h, g, 2, PACK)
         if first:
-            act += [("iv", h, 0, 1)] + [("ck", h, 2, b) for b in both] + [("iv", h, 1, b) for b in both]
-            act += [("ck", h, 3, b) for b in both] + [("iv", h, g, b) for g in (2, 3) for b in both]
+            for g in HALVES:
+                pe += tiles("multiply_k", h, g, 0, 3) + [("turn_k", h, g + 2, 0), ("multiply_k", h, g, 3), ("turn_k", h, g + 2, 1)]
+            act += [("interleave_v", h, 0, 1), ("interleave_v", h, 1, 0)] + both("copy_k", h, 2)
+            act += [("interleave_v", h, 1, 1)] + both("copy_k", h, 3)
+            act += both("interleave_v", h, 2) + both("interleave_v", h, 3)
         else:
-            act += [("ck", h, 2, 0), ("iv", h, 0, 1), ("co", h - 1, 2, 0), ("ck", h, 2, 1), ("iv", h, 1, 0), ("iv", h, 1, 1), ("co", h - 1, 3, 0)]
-            act += [("iv", h, 2, 0), ("ck", h, 3, 0), ("ck", h, 3, 1), ("iv", h, 2, 1), ("iv", h, 3, 0), ("iv", h, 3, 1)]
-        dve += [("sp", h, 3, 0), ("qv", h, 0), ("sp", h, 3, 1), ("qv", h, 1), ("sp", h, 3, 2), ("sp", h, 3, 3), ("rc", h, 0), ("qv", h, 2)]
-        dve += each("st", h, 0) + [("rc", h, 1), ("qv", h, 3)] + each("st", h, 1) + [("rc", h, 2)]
-        dve += weave(each("qw", h, 0), each("st", h, 2)) + [("rc", h, 3)]
-        pe += each("tw", h, 0) + [("off", h + 1)] * (not last) + [("warm", 3 + 2 * h, 2 * h)] + each("tw", h, 1)[:1] + [("warm", 4 + 2 * h, 2 * h)] + each("tw", h, 1)[1:] + weave(each("mo", h, 0), each("tw", h, 2))
+            pe += tiles("multiply_k", h, 0, 0, 3) + [("turn_k", h, 2, 0)] + parts("multiply_v", h - 1, 2)
+            pe += [("multiply_k", h, 0, 3), ("turn_k", h, 2, 1)]
+            pe += tiles("multiply_k", h, 1, 0, 3) + parts("multiply_v", h - 1, 3) + [("multiply_k", h, 1, 3)] + both("turn_k", h, 3)
+            act += [("copy_k", h, 2, 0), ("interleave_v", h, 0, 1), ("store_result", h - 1, 2, 0), ("copy_k", h, 2, 1)]
+            act += both("interleave_v", h, 1) + [("store_result", h - 1, 3, 0), ("interleave_v", h, 2, 0)] + both("copy_k", h, 3)
+            act += [("interleave_v", h, 2, 1)] + both("interleave_v", h, 3)
+        pe += tiles("multiply_k", h, 2, 0, PACK)
         if not last:
-            act += [("nb", h, 0), ("cq", h + 1, 0, 2), ("ex", h, 0), ("nb", h, 1), ("cq", h + 1, 2, 4), ("ex", h, 1), ("nb", h, 2), ("nb", h, 3)]
-            act += [("ex", h, 2)] + each("cw", h, 0) + [("coff", h + 1), ("ex", h, 3)] + each("cw", h, 1) + [("co", h, 0, 0)]
-            act += [("ck", h + 1, 0, 0), ("ck", h + 1, 0, 1)] + each("cw", h, 2)
-            act += [("co", h, 1, 0), ("ck", h + 1, 1, 0), ("ck", h + 1, 1, 1)] + each("cw", h, 3) + [("iv", h + 1, 0, 0)]
-            tail = each("st", h, 3)
-            dve += [("mq", h + 1, 0, 0, 4)] + each("qw", h, 1)[:1] + [tail[0]] + each("qw", h, 1)[1:] + [("qq", h + 1, 0), ("qk", h + 1, 0), tail[1]] + each("qw", h, 2)
-            pe += [("tk", h + 1, 0, b) for b in both] + each("mo", h, 1) + [("tk", h + 1, 1, b) for b in both] + each("tw", h, 3)
+            pe += [("turn_q", h + 1) + part for part in q_parts(h + 1)]
+        pe += tiles("multiply_k", h, 3, 0, PACK) + [("spread_v_scale", h, b) for b in HALVES]
+
+        values = [("quantize_v", h) + part for part in value_parts()]
+        weigh = [parts("weigh", h, i) for i in range(PACK)]
+        turn = [parts("turn_w", h, i) for i in range(PACK)]
+        copy = [parts("copy_w", h, i) for i in range(PACK)]
+        bias = [("exp_bias", h, i) for i in range(PACK)]
+        exp = [("exponentiate", h, i) for i in range(PACK)]
+        dve += tiles("take_scores", h, 3, 0, 1) + values[:1] + tiles("take_scores", h, 3, 1, PACK)
+        dve += [("invert_sum", h, 0), values[1]] + weigh[0] + [("invert_sum", h, 1), values[2]] + weigh[1]
+        dve += [("invert_sum", h, 2)] + weave(parts("quantize_w", h, 0), weigh[2]) + [("invert_sum", h, 3)]
+        if not last:
+            pe += turn[0] + [("offsets", h + 1)] + turn[1] + weave(parts("multiply_v", h, 0), turn[2])
+            pe += both("turn_k", h + 1, 0) + parts("multiply_v", h, 1) + both("turn_k", h + 1, 1) + turn[3]
+            next_q = [("copy_q", h + 1) + part for part in q_parts(h + 1)]
+            act += [next_q[0], bias[0], exp[0], bias[1], next_q[1], exp[1], bias[2], bias[3], exp[2]]
+            act += copy[0] + [("copy_offsets", h + 1), exp[3]] + copy[1] + [("store_result", h, 0, 0)]
+            act += both("copy_k", h + 1, 0) + copy[2] + [("store_result", h, 1, 0)] + both("copy_k", h + 1, 1)
+            act += copy[3] + [("interleave_v", h + 1, 0, 0)]
+            second = parts("quantize_w", h, 1)
+            dve += [("scale_q", h + 1, 0, 0, PACK), second[0], weigh[3][0], second[1]]
+            dve += [("quantize_qk", h + 1, 0), weigh[3][1]] + parts("quantize_w", h, 2)
         else:
-            act += [("nb", h, 0), ("ex", h, 0), ("nb", h, 1), ("nb", h, 2), ("ex", h, 1), ("nb", h, 3), ("ex", h, 2)]
-            act += each("cw", h, 0) + [("ex", h, 3)] + each("cw", h, 1) + [("co", h, 0, 0)] + each("cw", h, 2)
-            act += each("cw", h, 3)[:1] + [("co", h, 1, 0)] + each("cw", h, 3)[1:] + [("co", h, 2, 0), ("co", h, 3, 0), ("co", h, 3, 1)]
-            dve += each("qw", h, 1) + each("st", h, 3)[:1] + each("qw", h, 2) + each("st", h, 3)[1:] + each("qw", h, 3)[:1]
-            dve += [("io", h - 1, 0)] + each("qw", h, 3)[1:] + [("io", h - 1, 1), ("qo", h - 1, 0), ("qo", h - 1, 1)]
-            dve += [("io", h, 0), ("io", h, 1), ("qo", h, 0), ("qo", h, 1)]
-            pe += each("mo", h, 1) + each("tw", h, 3)[:1] + each("mo", h, 2) + each("tw", h, 3)[1:] + each("mo", h, 3)
+            pe += turn[0] + [("warm", 3, 2), turn[1][0], ("warm", 4, 2), turn[1][1]] + weave(parts("multiply_v", h, 0), turn[2])
+            pe += parts("multiply_v", h, 1) + turn[3][:1] + parts("multiply_v", h, 2) + turn[3][1:] + parts("multiply_v", h, 3)
+            act += [bias[0], exp[0], bias[1], bias[2], exp[1], bias[3], exp[2]]
+            act += copy[0] + [exp[3]] + copy[1] + copy[2] + [("store_result", h, 0, 0)]
+            act += copy[3][:1] + [("store_result", h, 1, 0)] + copy[3][1:] + [("store_result", h, 2, 0)]
+            act += both("store_result", h, 3)
+            final = parts("quantize_w", h, 3)
+            dve += parts("quantize_w", h, 1) + weigh[3][:1] + parts("quantize_w", h, 2) + weigh[3][1:]
+            dve += [final[0], ("round_result", h - 1, 0)] + final[1:] + [("round_result", h - 1, 1), ("store_planes", h - 1, 0)]
+            dve += [("round_result", h, c) for c in HALVES] + [("store_planes", h, c) for c in HALVES]
     return pe, act, dve
 
 
 def producers(step):
     name, args = step[0], step[1:]
-    both = (0, 1)
     table = {
-        "cz": lambda: [("tz",)],
-        "cq": lambda h, i0, i1: [("tq", h, i0, i1)],
-        "ck": lambda h, g, b: [("tk", h, g, b)],
-        "off": lambda h: [("cz",)] + [("cq", h) + part for part in q_parts(h)],
-        "coff": lambda h: [("off", h)],
-        "mq": lambda h, g, i0, i1: [("cz",)] + [("cq", h) + part for part in q_parts(h) if i0 <= part[0] < i1],
-        "qq": lambda h, g: [("mq", h, g, 3 if (h, g) == (0, 0) else 0, 4)],
-        "bv": lambda h, b: [("cz",)],
-        "qk": lambda h, g: [("ck", h, g, b) for b in both],
-        "qv": lambda h, g: [("iv", h, g, b) for b in both],
-        "ms": lambda h, g, i: [("qq", h, g), ("qk", h, g)],
-        "sp": lambda h, g, i: [("ms", h, g, i), ("coff", h)],
-        "nb": lambda h, i: [("sp", h, G - 1, i)],
-        "ex": lambda h, i: [("nb", h, i)],
-        "rc": lambda h, i: [("ex", h, i)],
-        "st": lambda h, i, g0, g1: [("rc", h, i), ("bv", h, g0 // 2)],
-        "tw": lambda h, i, g0, g1: [("st", h, i, g0, g1)],
-        "cw": lambda h, i, g0, g1: [("tw", h, i, g0, g1)],
-        "qw": lambda h, i, g0, g1: [("cw", h, i, g0, g1)],
-        "mo": lambda h, i, g0, g1: [("qw", h, i, g0, g1)] + [("qv", h, g) for g in range(g0, g1)],
-        "co": lambda h, i, c: [("mo", h, i) + pieces(h, i)[-1]],
-        "io": lambda h, c: [("co", h, i, 0) for i in range(PACK - 1)] + [("co", h, PACK - 1, c if h == H - 1 else 0)],
-        "qo": lambda h, c: [("io", h, c)],
+        "copy_factors": lambda: [("turn_factors",)],
+        "copy_q": lambda h, i0, i1: [("turn_q", h, i0, i1)],
+        "copy_k": lambda h, g, b: [("turn_k", h, g, b)],
+        "offsets": lambda h: [("copy_factors",)] + [("copy_q", h) + part for part in q_parts(h)],
+        "copy_offsets": lambda h: [("offsets", h)],
+        "scale_q": lambda h, g, i0, i1: [("copy_factors",)] + [("copy_q", h) + part for part in q_parts(h) if i0 <= part[0] < i1],
+        "quantize_qk": lambda h, g: [("scale_q", h, g, PACK - 1 if (h, g) == (0, 0) else 0, PACK)]
+        + [("copy_k", h, g, b) for b in HALVES],
+        "quantize_v": lambda h, g0, g1: [("interleave_v", h, g, b) for g in range(g0, g1) for b in HALVES],
+        "multiply_k": lambda h, g, i: [("quantize_qk", h, g)],
+        "take_scores": lambda h, g, i: [("multiply_k", h, g, i), ("copy_offsets", h)],
+        "exp_bias": lambda h, i: [("take_scores", h, G - 1, i)],
+        "exponentiate": lambda h, i: [("exp_bias", h, i)],
+        "invert_sum": lambda h, i: [("exponentiate", h, i)],
+        "weigh": lambda h, i, g0, g1: [("invert_sum", h, i), ("spread_v_scale", h, g0 // 2)],
+        "turn_w": lambda h, i, g0, g1: [("weigh", h, i, g0, g1)],
+        "copy_w": lambda h, i, g0, g1: [("turn_w", h, i, g0, g1)],
+        "quantize_w": lambda h, i, g0, g1: [("copy_w", h, i) + part for part in weight_parts(h, i) if g0 <= part[0] < g1],
+        "multiply_v": lambda h, i, g0, g1: [("quantize_w", h, i, g0, g1)] + [("quantize_v", h) + part for part in value_parts()],
+        "store_result": lambda h, i, c: [("multiply_v", h, i) + product_parts(h, i)[-1]],
+        "round_result": lambda h, c: [("store_result", h, i, c if (h, i) == LAST_TILE else 0) for i in range(PACK)],
+        "store_planes": lambda h, c: [("round_result", h, c)] if h == H - 1 else [("round_result", h, b) for b in HALVES],
     }
     return table[name](*args) if name in table else []
 
@@ -140,7 +166,7 @@ def producers(step):
 def schedule():
     queues = [list(order) for order in engine_orders()]
     written, text = set(), []
-    for turn in range(sum(len(order) for order in queues)):
+    for place in range(sum(len(order) for order in queues)):
         ready = [order for order in queues if order and all(p in written for p in producers(order[0]))]
         step = ready[0][0]
         ready[0].remove(step)
@@ -152,35 +178,38 @@ def schedule():
 def tile_kivigroupedscalefoldedattention_x1_kernel(tc, q, k_code, k_scale, k_zero, v_code, v_scale, out_0, out_1, out_2):
     nc = tc.nc
     with ExitStack() as ctx:
-        keep = ctx.enter_context(tc.tile_pool(name="keep", bufs=1))
-        stage = ctx.enter_context(tc.tile_pool(name="stage", bufs=3))
+        sbuf = ctx.enter_context(tc.tile_pool(name="sbuf", bufs=1))
         banks = ctx.enter_context(tc.psum_pool(name="banks", bufs=1))
-        turn_pool = ctx.enter_context(tc.psum_pool(name="turn", bufs=4))
+        turn_banks = ctx.enter_context(tc.psum_pool(name="turn", bufs=TRANSPOSE_BANKS))
         ctx.enter_context(tc.manual_schedule())
 
+        def rotating(tag, bufs, shape, dtype):
+            return sbuf.tile(shape, dtype, name=tag, tag=tag, bufs=bufs, align_bytes=64)
+
         def kept(name, shape, dtype):
-            return keep.tile(shape, dtype, name=name, align_bytes=64)
+            return rotating(name, 1, shape, dtype)
 
         def staged(tag, shape, dtype):
-            return stage.tile(shape, dtype, name=tag, tag=tag, align_bytes=64)
+            return rotating(tag, 3, shape, dtype)
+
+        def per_head(tag, shape, dtype):
+            return rotating(tag, 4, shape, dtype)
 
         def bank_tile(number, shape, dtype):
             return banks.tile(shape, dtype, name="bank%d" % number, tag="bank%d" % number)
 
-        def per_head(tag, shape, dtype):
-            return stage.tile(shape, dtype, name=tag, tag=tag, bufs=4, align_bytes=64)
-
+        rows = H * G
         factor_rows = kept("factor_rows", [P, D], BF16)
         nc.gpsimd.memset(factor_rows[:].bitcast(I32), 0)
-        nc.scalar.dma_start(out=factor_rows[0 : H * G, :], in_=k_scale.rearrange("h g d -> (h g) d"))
-        nc.scalar.dma_start(out=factor_rows[H * G : 2 * H * G, :], in_=k_zero.rearrange("h g d -> (h g) d"))
-        nc.scalar.dma_start(out=factor_rows[2 * H * G : 3 * H * G, :], in_=v_scale.rearrange("h (g t) -> (h g) t", g=G))
+        nc.scalar.dma_start(out=factor_rows[0:rows, :], in_=k_scale.rearrange("h g d -> (h g) d"))
+        nc.scalar.dma_start(out=factor_rows[rows : 2 * rows, :], in_=k_zero.rearrange("h g d -> (h g) d"))
+        nc.scalar.dma_start(out=factor_rows[2 * rows : 3 * rows, :], in_=v_scale.rearrange("h (g t) -> (h g) t", g=G))
         ident = kept("ident", [P, P], F32)
         make_identity(nc, ident[:])
-        pick = kept("pick", [P, H * G], BF16)
-        nc.gpsimd.tensor_copy(out=pick[:], in_=ident[:, 2 * H * G : 3 * H * G])
-        warm = kept("warm", [P, 1], F32)
-        nc.scalar.activation(out=warm[:], in_=ident[:, 0:1], func=ACT.Exp)
+        pick = kept("pick", [P, rows], BF16)
+        nc.gpsimd.tensor_copy(out=pick[:], in_=ident[:, 2 * rows : 3 * rows])
+        exp_warm = kept("exp_warm", [P, 1], F32)
+        nc.scalar.activation(out=exp_warm[:], in_=ident[:, 0:1], func=ACT.Exp)
 
         q_rows, k_rows, v_rows = {}, {}, {}
 
@@ -192,9 +221,9 @@ def tile_kivigroupedscalefoldedattention_x1_kernel(tc, q, k_code, k_scale, k_zer
 
         def load_k(h, g):
             src = k_code[h, g].rearrange("(p j) d -> p j d", j=PACK)
-            for b in range(2):
-                k_rows[h, g, b] = kept("k_rows%d%d%d" % (h, g, b), [P, 2, D], BF16)
-                nc.sync.dma_start(out=k_rows[h, g, b][:], in_=src[:, 2 * b : 2 * b + 2, :])
+            for u in HALVES:
+                k_rows[h, g, u] = kept("k_rows%d%d%d" % (h, g, u), [P, 2, D], BF16)
+                nc.sync.dma_start(out=k_rows[h, g, u][:], in_=src[:, 2 * u : 2 * u + 2, :])
 
         def load_v(h, g):
             v_rows[h, g] = per_head("v_rows", [P, PACK, D], BF16)
@@ -203,178 +232,175 @@ def tile_kivigroupedscalefoldedattention_x1_kernel(tc, q, k_code, k_scale, k_zer
         load_q(0)
         load_k(0, 0)
         for h in range(H):
-            load_k(h, 1)
-            load_v(h, 0)
-            load_k(h, 2)
-            load_v(h, 1)
-            load_k(h, 3)
-            load_v(h, 2)
-            load_v(h, 3)
+            for g in range(G):
+                if g + 1 < G:
+                    load_k(h, g + 1)
+                load_v(h, g)
             if h + 1 < H:
                 load_q(h + 1)
                 load_k(h + 1, 0)
 
-        factors = kept("factors", [P, 2 * H * G, PACK], BF16)
-        q_t = {h: kept("q_t%d" % h, [P, N, PACK], BF16) for h in range(H)}
-        offs = {h: kept("offs%d" % h, [P, PACK, G], F32) for h in range(H)}
+        factors = kept("factors", [P, 2 * rows, PACK], BF16)
+        q_turned = {h: kept("q_turned%d" % h, [P, N, PACK], BF16) for h in range(H)}
+        off = {h: kept("off%d" % h, [P, PACK, G], F32) for h in range(H)}
         run_max = {h: kept("run_max%d" % h, [P, PACK, G], F32) for h in range(H)}
-        exp_bias = {h: kept("exp_bias%d" % h, [P, PACK], F32) for h in range(H)}
+        neg_max = {h: kept("neg_max%d" % h, [P, PACK], F32) for h in range(H)}
         row_sum = {h: kept("row_sum%d" % h, [P, PACK], F32) for h in range(H)}
         row_inv = {h: kept("row_inv%d" % h, [P, PACK], F32) for h in range(H)}
-        scores = {}
         result = {h: kept("result%d" % h, [P, PACK, D], F32) for h in range(H)}
+        rounded = {h: kept("rounded%d" % h, [P, D, PACK], BF16) for h in range(H)}
+        out_codes = kept("out_codes", [P, H * D], U32)
+        out_scales = kept("out_scales", [P, H * D], U8)
+        zeros = kept("zeros", [P, W], BF16)
+        nc.vector.memset(zeros[:].bitcast(I32), 0)
         live = {}
 
-        def words(tile_ap):
-            return tile_ap.bitcast(F32)
+        def as_words(packed):
+            return packed.rearrange("p c j -> p (c j)").bitcast(F32)
 
-        def turn(key, sources, step=2):
-            bank = turn_pool.tile([P, len(sources), 2, P], F32, name="turn_bank", tag="turn_bank")
-            for r, src in enumerate(sources):
-                for u in range(2):
-                    nc.tensor.transpose(bank[:, r, u, :], src[:, u : 2 * P : 2] if step == 2 else src[:, u * P : (u + 1) * P], ident[:])
+        def turn(key, sources, alternate):
+            bank = turn_banks.tile([P, len(sources), 2, P], F32, name="turn_bank", tag="turn_bank")
+            for r, source in enumerate(sources):
+                words = source.bitcast(F32)
+                for u in HALVES:
+                    chosen = words[:, u : 2 * P : 2] if alternate else words[:, u * P : (u + 1) * P]
+                    nc.tensor.transpose(bank[:, r, u, :], chosen, ident[:])
             live[key] = bank
 
-        def turn_out(key, dst, engine):
-            src = live[key][:].rearrange("p r u m -> p r m u")
-            view = dst.rearrange("p c j -> p (c j)").bitcast(F32).rearrange("p (r m u) -> p r m u", m=P, u=2)
-            if engine == "v":
-                nc.vector.tensor_copy(out=view, in_=src)
-            else:
-                nc.scalar.copy(out=view, in_=src)
+        def copy_turned(key, packed):
+            dst = as_words(packed).rearrange("p (r m u) -> p r m u", m=P, u=2)
+            nc.scalar.copy(out=dst, in_=live[key][:].rearrange("p r u m -> p r m u"))
 
-        def quantize(key, pool_fn, tag, src):
-            codes = pool_fn(tag + "_codes", [P, src.shape[1]], U32)
-            scales = pool_fn(tag + "_scales", [P, src.shape[1]], U8)
-            nc.vector.quantize_mx(out=codes[:].bitcast(FP8X4), scales=scales[:], in_=src.rearrange("p c j -> p (c j)"))
-            live[key] = (codes, scales)
+        def interleave(copy, packed, source):
+            copy(out=packed.rearrange("p (c i) j -> p c j i", i=4), in_=source.rearrange("p j (c i) -> p c j i", i=4))
 
-        def mx(out, stationary, cols, moving, moving_cols, start, stop):
+        def quantize(codes, scales, packed):
+            nc.vector.quantize_mx(out=codes.bitcast(FP8X4), scales=scales, in_=packed.rearrange("p c j -> p (c j)"))
+
+        def quantize_new(key, make_tile, tag, packed):
+            live[key] = (make_tile(tag + "_codes", [P, packed.shape[1]], U32), make_tile(tag + "_scales", [P, packed.shape[1]], U8))
+            quantize(live[key][0][:], live[key][1][:], packed)
+
+        def multiply(out, stationary, stationary_cols, moving, moving_cols, start, stop):
             nc.tensor.matmul_mx(
                 out=out,
-                lhsT=stationary[0][:, cols].bitcast(FP8X4),
-                lhsT_scale=stationary[1][:, cols],
+                lhsT=stationary[0][:, stationary_cols].bitcast(FP8X4),
+                lhsT_scale=stationary[1][:, stationary_cols],
                 rhs=moving[0][:, moving_cols].bitcast(FP8X4),
                 rhs_scale=moving[1][:, moving_cols],
                 start=start,
                 stop=stop,
             )
 
-        zeros = kept("zeros", [P, W], BF16)
-        nc.vector.memset(zeros[:].bitcast(I32), 0)
-
-        def warm_pass(n, count):
-            if count:
-                idle_bank = bank_tile(2 if n < 3 else 3, [P, W], F32)
+        def warm(number, count):
+            idle_bank = bank_tile(SCORE_BANKS - 1 if number < 3 else RESULT_BANK, [P, W], F32)
             for repeat in range(count):
                 nc.tensor.matmul(idle_bank[:], lhsT=zeros[:, 0:P], rhs=zeros[:], start=True, stop=True)
 
-        def tz():
-            bank = bank_tile(3, [P, 2, P], F32)
-            for u in range(2):
-                nc.tensor.transpose(bank[:, u, :], words(factor_rows[:])[:, u : 2 * P : 2], ident[:])
-            live["z"] = bank
+        def turn_factors():
+            bank = bank_tile(RESULT_BANK, [P, 2, P], F32)
+            for u in HALVES:
+                nc.tensor.transpose(bank[:, u, :], factor_rows[:].bitcast(F32)[:, u : 2 * P : 2], ident[:])
+            live["factors"] = bank
 
-        def cz():
+        def copy_factors():
             nc.vector.tensor_copy(
-                out=factors[:].rearrange("p r j -> p (r j)").bitcast(F32).rearrange("p (r u) -> p r u", u=2),
-                in_=live["z"][:, :, 0 : 2 * H * G].rearrange("p u r -> p r u"),
+                out=as_words(factors[:]).rearrange("p (r u) -> p r u", u=2),
+                in_=live["factors"][:, :, 0 : 2 * rows].rearrange("p u r -> p r u"),
             )
 
-        def tq(h, i0, i1):
-            turn(("q", h, i0), [words(q_rows[h, i0][:, r, :]) for r in range(i1 - i0)])
+        def turn_q(h, i0, i1):
+            turn(("q", h, i0), [q_rows[h, i0][:, r, :] for r in range(i1 - i0)], True)
 
-        def cq(h, i0, i1):
-            turn_out(("q", h, i0), q_t[h][:, P * i0 : P * i1, :], "s")
+        def copy_q(h, i0, i1):
+            copy_turned(("q", h, i0), q_turned[h][:, P * i0 : P * i1, :])
 
-        def tk(h, g, b):
-            turn(("k", h, g, b), [words(k_rows[h, g, b][:, r, :]) for r in range(2)])
+        def qk_tile(h, g):
+            if ("qk", h, g) not in live:
+                live["qk", h, g] = per_head("qk", [P, N + W, PACK], BF16)
+            return live["qk", h, g]
 
-        def ck(h, g, b):
-            if b == 0:
-                live["kt", h, g] = staged("k_t", [P, W, PACK], BF16)
-            dst = live["kt", h, g][:, 2 * P * b : 2 * P * (b + 1), :].rearrange("p c j -> p (c j)").bitcast(F32)
-            nc.scalar.copy(out=dst.rearrange("p (m e u) -> p m e u", e=2, u=2), in_=live["k", h, g, b][:].rearrange("p e u m -> p m e u"))
+        def turn_k(h, g, u):
+            turn(("k", h, g, u), [k_rows[h, g, u][:, e, :] for e in HALVES], True)
 
-        def off(h):
-            bank = bank_tile(3, [P, PACK, G], F32)
-            first = H * G + h * G
+        def copy_k(h, g, u):
+            dst = as_words(qk_tile(h, g)[:, N + 2 * P * u : N + 2 * P * (u + 1), :]).rearrange("p (m e w) -> p m e w", e=2, w=2)
+            nc.scalar.copy(out=dst, in_=live["k", h, g, u][:].rearrange("p e w m -> p m e w"))
+
+        def offsets(h):
+            bank = bank_tile(RESULT_BANK, [P, PACK, G], F32)
+            zero_rows = slice(rows + h * G, rows + (h + 1) * G)
             for i in range(PACK):
                 for j in range(PACK):
                     nc.tensor.matmul(
                         bank[:, i, :],
-                        lhsT=q_t[h][:, i * P : (i + 1) * P, j],
-                        rhs=factors[:, first : first + G, j],
+                        lhsT=q_turned[h][:, i * P : (i + 1) * P, j],
+                        rhs=factors[:, zero_rows, j],
                         start=(j == 0),
                         stop=(j == PACK - 1),
                     )
             live["off", h] = bank
 
-        def coff(h):
-            nc.scalar.copy(out=offs[h][:], in_=live["off", h][:])
+        def copy_offsets(h):
+            nc.scalar.copy(out=off[h][:], in_=live["off", h][:])
 
-        def mq(h, g, i0, i1):
-            if i0 == 0:
-                live["qs", h, g] = staged("qs", [P, N, PACK], BF16)
-            rows = slice(i0 * P, i1 * P)
+        def scale_q(h, g, i0, i1):
+            cols = slice(i0 * P, i1 * P)
             factor = factors[:, h * G + g : h * G + g + 1, :].to_broadcast([P, (i1 - i0) * P, PACK])
-            nc.vector.tensor_tensor(out=live["qs", h, g][:, rows, :], in0=q_t[h][:, rows, :], in1=factor, op=ALU.mult)
+            nc.vector.tensor_tensor(out=qk_tile(h, g)[:, cols, :], in0=q_turned[h][:, cols, :], in1=factor, op=ALU.mult)
 
-        def qq(h, g):
-            quantize(("qq", h, g), staged, "qs", live["qs", h, g][:])
+        def quantize_qk(h, g):
+            quantize_new(("qk_mx", h, g), staged, "qk", qk_tile(h, g)[:])
 
-        def qk(h, g):
-            quantize(("qk", h, g), staged, "k", live["kt", h, g][:])
+        def interleave_v(h, g, c):
+            g0, g1 = [part for part in value_parts() if part[0] <= g < part[1]][0]
+            if (g, c) == (g0, 0):
+                live["v", h, g0] = kept("v_packed%d" % g0, [P, (g1 - g0) * D, PACK], BF16)
+            cols = channel_parts(True)[c]
+            first = (g - g0) * D
+            interleave(nc.scalar.copy, live["v", h, g0][:, first + cols.start : first + cols.stop, :], v_rows[h, g][:, :, cols])
 
-        def iv(h, g, b):
-            if b == 0:
-                live["vt", h, g] = per_head("v_t", [P, D, PACK], BF16)
-            cols = slice(b * D // 2, (b + 1) * D // 2)
-            nc.scalar.copy(
-                out=live["vt", h, g][:, cols, :].rearrange("p (c i) j -> p c j i", i=4),
-                in_=v_rows[h, g][:, :, cols].rearrange("p j (c i) -> p c j i", i=4),
-            )
+        def quantize_v(h, g0, g1):
+            quantize_new(("v_mx", h, g0), kept, "v%d" % g0, live["v", h, g0][:])
 
-        def qv(h, g):
-            quantize(("qv", h, g), per_head, "v", live["vt", h, g][:])
+        def multiply_k(h, g, i):
+            bank = bank_tile((g * PACK + i) % SCORE_BANKS, [P, W], F32)
+            operands = live["qk_mx", h, g]
+            multiply(bank[:], operands, slice(i * P, (i + 1) * P), operands, slice(N, N + W), True, True)
+            live["scores_bank", h, g, i] = bank
 
-        def ms(h, g, i):
-            bank = bank_tile((g * PACK + i) % 3, [P, W], F32)
-            mx(bank[:], live["qq", h, g], slice(i * P, (i + 1) * P), live["qk", h, g], slice(0, W), True, True)
-            live["s", h, g, i] = bank
-
-        def sp(h, g, i):
+        def take_scores(h, g, i):
             if g == 0:
-                scores[h, i] = per_head("scores", [P, T], F32)
+                live["scores", h, i] = per_head("scores", [P, T], F32)
             nc.vector.tensor_scalar(
-                out=scores[h, i][:, g * W : (g + 1) * W],
-                in0=live["s", h, g, i][:],
-                scalar1=offs[h][:, i, g : g + 1],
+                out=live["scores", h, i][:, g * W : (g + 1) * W],
+                in0=live["scores_bank", h, g, i][:],
+                scalar1=off[h][:, i, g : g + 1],
                 scalar2=run_max[h][:, i, g - 1 : g] if g > 0 else None,
                 op0=ALU.add,
                 op1=ALU.max,
                 accum_out=run_max[h][:, i, g : g + 1],
             )
 
-        def nb(h, i):
-            nc.scalar.activation(out=exp_bias[h][:, i : i + 1], in_=run_max[h][:, i, G - 1 : G], func=ACT.Copy, scale=-SOFTMAX_SCALE)
+        def exp_bias(h, i):
+            nc.scalar.activation(out=neg_max[h][:, i : i + 1], in_=run_max[h][:, i, G - 1 : G], func=ACT.Copy, scale=-SOFTMAX_SCALE)
 
-        def ex(h, i):
+        def exponentiate(h, i):
             nc.scalar.activation(
-                out=scores[h, i][:],
-                in_=scores[h, i][:],
+                out=live["scores", h, i][:],
+                in_=live["scores", h, i][:],
                 func=ACT.Exp,
-                bias=exp_bias[h][:, i : i + 1],
+                bias=neg_max[h][:, i : i + 1],
                 scale=SOFTMAX_SCALE,
                 accum_out=row_sum[h][:, i : i + 1],
             )
 
-        def rc(h, i):
+        def invert_sum(h, i):
             nc.vector.reciprocal(out=row_inv[h][:, i : i + 1], in_=row_sum[h][:, i : i + 1])
 
-        def bv(h, b):
-            bank = bank_tile(1 + b, [P, 2, W], BF16)
-            for r in range(2):
+        def spread_v_scale(h, b):
+            bank = bank_tile(V_SCALE_BANK + b, [P, 2, W], BF16)
+            for r in HALVES:
                 row = h * G + 2 * b + r
                 nc.tensor.matmul(
                     bank[:, r, :],
@@ -383,77 +409,71 @@ def tile_kivigroupedscalefoldedattention_x1_kernel(tc, q, k_code, k_scale, k_zer
                     start=True,
                     stop=True,
                 )
-            live["vs", h, b] = bank
+            live["v_scale", h, b] = bank
 
-        def st(h, i, g0, g1):
+        def weigh(h, i, g0, g1):
             ws = per_head("ws", [P, (g1 - g0) * W], BF16)
-            cols = slice(g0 * W, g1 * W)
-            vs = live["vs", h, g0 // 2][:, g0 % 2 : g0 % 2 + g1 - g0, :].rearrange("p r t -> p (r t)")
             nc.vector.scalar_tensor_tensor(
-                out=ws[:], in0=scores[h, i][:, cols], scalar=row_inv[h][:, i : i + 1], in1=vs, op0=ALU.mult, op1=ALU.mult
+                out=ws[:],
+                in0=live["scores", h, i][:, g0 * W : g1 * W],
+                scalar=row_inv[h][:, i : i + 1],
+                in1=live["v_scale", h, g0 // 2][:, g0 % 2 : g0 % 2 + g1 - g0, :].rearrange("p r t -> p (r t)"),
+                op0=ALU.mult,
+                op1=ALU.mult,
             )
             live["ws", h, i, g0] = ws
 
-        def tw(h, i, g0, g1):
-            ws = live["ws", h, i, g0]
-            turn(("w", h, i, g0), [words(ws[:, r * W : (r + 1) * W]) for r in range(g1 - g0)], step=1)
+        def turn_w(h, i, g0, g1):
+            turn(("w", h, i, g0), [live["ws", h, i, g0][:, r * W : (r + 1) * W] for r in range(g1 - g0)], False)
 
-        def cw(h, i, g0, g1):
-            live["wt", h, i, g0] = per_head("w_t", [P, (g1 - g0) * P, PACK], BF16)
-            turn_out(("w", h, i, g0), live["wt", h, i, g0][:], "s")
+        def copy_w(h, i, g0, g1):
+            c0, c1 = [part for part in product_parts(h, i) if part[0] <= g0 < part[1]][0]
+            if g0 == c0:
+                live["w_packed", h, i, c0] = staged("w_packed", [P, (c1 - c0) * P, PACK], BF16)
+            copy_turned(("w", h, i, g0), live["w_packed", h, i, c0][:, (g0 - c0) * P : (g1 - c0) * P, :])
 
-        def qw(h, i, g0, g1):
-            quantize(("qw", h, i, g0), per_head, "w", live["wt", h, i, g0][:])
+        def quantize_w(h, i, g0, g1):
+            quantize_new(("w_mx", h, i, g0), per_head, "w", live["w_packed", h, i, g0][:])
 
-        def out_parts(h, i):
-            if (h, i) == (H - 1, PACK - 1):
-                return [slice(0, D // 2), slice(D // 2, D)]
-            return [slice(0, D)]
-
-        def mo(h, i, g0, g1):
-            parts = out_parts(h, i)
-            for c, cols in enumerate(parts):
+        def multiply_v(h, i, g0, g1):
+            for c, cols in enumerate(channel_parts((h, i) == LAST_TILE)):
                 if g0 == 0:
-                    live["o", h, i, c] = bank_tile(c if h == H - 1 and i % 2 else 3, [P, D // len(parts)], F32)
+                    number = c if h == H - 1 and i % 2 else RESULT_BANK
+                    live["result_bank", h, i, c] = bank_tile(number, [P, cols.stop - cols.start], F32)
                 for g in range(g0, g1):
-                    mx(live["o", h, i, c][:], live["qw", h, i, g0], slice((g - g0) * P, (g - g0 + 1) * P), live["qv", h, g], cols,
-                       g == 0, g == G - 1)
+                    v0 = [part[0] for part in value_parts() if part[0] <= g < part[1]][0]
+                    v_cols = slice((g - v0) * D + cols.start, (g - v0) * D + cols.stop)
+                    w_cols = slice((g - g0) * P, (g - g0 + 1) * P)
+                    multiply(live["result_bank", h, i, c][:], live["w_mx", h, i, g0], w_cols, live["v_mx", h, v0], v_cols, g == 0, g == G - 1)
 
-        def co(h, i, c):
-            parts = out_parts(h, i)
-            nc.scalar.copy(out=result[h][:, i, parts[c]], in_=live["o", h, i, c][:])
-            if c == len(parts) - 1:
+        def store_result(h, i, c):
+            split = channel_parts((h, i) == LAST_TILE)
+            nc.scalar.copy(out=result[h][:, i, split[c]], in_=live["result_bank", h, i, c][:])
+            if c == len(split) - 1:
                 nc.sync.dma_start(out=out_0[h].rearrange("(p j) d -> p j d", j=PACK)[:, i, :], in_=result[h][:, i, :])
 
-        def io(h, c):
-            rounded = kept("rounded%d%d" % (h, c), [P, D // 2, PACK], BF16)
-            nc.vector.tensor_copy(
-                out=rounded[:].rearrange("p (c i) j -> p c j i", i=4),
-                in_=result[h][:, :, c * D // 2 : (c + 1) * D // 2].rearrange("p j (c i) -> p c j i", i=4),
-            )
-            live["r", h, c] = rounded
+        def round_result(h, c):
+            cols = channel_parts(True)[c]
+            interleave(nc.vector.tensor_copy, rounded[h][:, cols, :], result[h][:, :, cols])
 
-        out_codes = kept("out_codes", [P, H * D], U32)
-        out_scales = kept("out_scales", [P, H * D], U8)
+        def store_planes(h, c):
+            cols = channel_parts(h == H - 1)[c]
+            plane_cols = slice(h * D + cols.start, h * D + cols.stop)
+            quantize(out_codes[:, plane_cols], out_scales[:, plane_cols], rounded[h][:, cols, :])
+            out_words = out_1[0].rearrange("p m t -> p (m t)").bitcast(I32)
+            nc.sync.dma_start(out=out_words[:, plane_cols], in_=out_codes[:, plane_cols].bitcast(I32))
+            if plane_cols.stop == H * D:
+                for a in range(4):
+                    queue = nc.sync if a % 2 else nc.scalar
+                    queue.dma_start(out=out_2[0, 4 * a : 4 * a + 4, :].bitcast(I32), in_=out_scales[32 * a : 32 * a + 4, :].bitcast(I32))
 
-        def qo(h, c):
-            cols = slice(h * D + c * D // 2, h * D + (c + 1) * D // 2)
-            nc.vector.quantize_mx(
-                out=out_codes[:, cols].bitcast(FP8X4), scales=out_scales[:, cols], in_=live["r", h, c][:].rearrange("p c j -> p (c j)")
-            )
-            if c == 1:
-                head = slice(h * D, (h + 1) * D)
-                out_words = out_1[0].rearrange("p m t -> p (m t)").bitcast(I32)
-                nc.sync.dma_start(out=out_words[:, head], in_=out_codes[:, head].bitcast(I32))
-            if c == 1 and h == H - 1:
-                for quad in range(4):
-                    (nc.scalar if quad % 2 else nc.sync).dma_start(
-                        out=out_2[0, 4 * quad : 4 * quad + 4, :].bitcast(I32),
-                        in_=out_scales[32 * quad : 32 * quad + 4, :].bitcast(I32),
-                    )
-
-        steps = {"tz": tz, "cz": cz, "tq": tq, "cq": cq, "tk": tk, "ck": ck, "off": off, "coff": coff, "mq": mq, "warm": warm_pass, "bv": bv, "qq": qq, "qk": qk,
-                 "iv": iv, "qv": qv, "ms": ms, "sp": sp, "nb": nb, "ex": ex, "rc": rc, "st": st, "tw": tw, "cw": cw, "qw": qw,
-                 "mo": mo, "co": co, "io": io, "qo": qo}
-        for op in schedule():
-            steps[op[0]](*op[1:])
+        steps = {
+            "warm": warm, "turn_factors": turn_factors, "copy_factors": copy_factors, "turn_q": turn_q, "copy_q": copy_q,
+            "turn_k": turn_k, "copy_k": copy_k, "offsets": offsets, "copy_offsets": copy_offsets, "scale_q": scale_q,
+            "quantize_qk": quantize_qk, "interleave_v": interleave_v, "quantize_v": quantize_v, "multiply_k": multiply_k,
+            "take_scores": take_scores, "exp_bias": exp_bias, "exponentiate": exponentiate, "invert_sum": invert_sum,
+            "spread_v_scale": spread_v_scale, "weigh": weigh, "turn_w": turn_w, "copy_w": copy_w, "quantize_w": quantize_w,
+            "multiply_v": multiply_v, "store_result": store_result, "round_result": round_result, "store_planes": store_planes,
+        }
+        for step in schedule():
+            steps[step[0]](*step[1:])

@@ -32,6 +32,10 @@ def q_parts(h):
     return [(i, i + 1) for i in range(PACK)] if h == 0 else [(0, 2), (2, 4)]
 
 
+def offset_parts(h):
+    return [(0, 2), (2, 4)] if h == 0 else [(0, PACK)]
+
+
 def weight_parts(h, i):
     return [(0, 2), (2, 3), (3, 4)] if (h, i) == LAST_TILE else [(0, 2), (2, 4)]
 
@@ -66,26 +70,31 @@ def engine_orders():
 
     first_q = [("turn_q", 0) + part for part in q_parts(0)]
     pe += [("warm", 0, 3), first_q[0], ("turn_factors",)] + first_q[1:]
-    pe += [("warm", 1, 2)] + both("turn_k", 0, 0) + [("warm", 2, 2), ("offsets", 0)] + both("turn_k", 0, 1)
+    pe += [("warm", 1, 2)] + both("turn_k", 0, 0) + [("warm", 2, 2)] + both("turn_k", 0, 1)
+    pe += [("warm", 3, 2), ("offsets", 0, 0, 2)] + tiles("multiply_k", 0, 0, 0, 2) + [("offsets", 0, 2, 4), ("multiply_k", 0, 0, 2)]
     act += [("copy_q", 0) + part for part in q_parts(0)] + both("copy_k", 0, 0)
-    act += [("interleave_v", 0, 0, 0), ("copy_offsets", 0)] + both("copy_k", 0, 1)
+    act += [("interleave_v", 0, 0, 0)] + both("copy_k", 0, 1)
+    act += [("copy_offsets", 0, 0, 2), ("interleave_v", 0, 0, 1), ("copy_offsets", 0, 2, 4)]
     dve += [("copy_factors",)] + [("scale_q", 0, 0) + part for part in q_parts(0)]
     dve += [("scale_q", 0, 1, 0, PACK), ("scale_q", 0, 2, 0, PACK), ("quantize_qk", 0, 0), ("scale_q", 0, 3, 0, PACK)]
+    dve += [("quantize_qk", 0, 1)]
 
     for h in range(H):
         first, last = h == 0, h == H - 1
 
         for g in range(G - 1):
-            if not first:
-                dve += [("scale_q", h, g + 1, 0, PACK)]
+            if not first and g + 2 < G:
+                dve += [("scale_q", h, g + 2, 0, PACK)]
             dve += tiles("take_scores", h, g, 0, 2)
             if not first and g == 0:
                 dve += parts("quantize_w", h - 1, 3)
-            dve += [("quantize_qk", h, g + 1)] + tiles("take_scores", h, g, 2, PACK)
+            if (h, g) != (0, 0):
+                dve += [("quantize_qk", h, g + 1)]
+            dve += tiles("take_scores", h, g, 2, PACK)
         if first:
-            for g in HALVES:
-                pe += tiles("multiply_k", h, g, 0, 3) + [("turn_k", h, g + 2, 0), ("multiply_k", h, g, 3), ("turn_k", h, g + 2, 1)]
-            act += [("interleave_v", h, 0, 1), ("interleave_v", h, 1, 0)] + both("copy_k", h, 2)
+            pe += [("turn_k", h, 2, 0), ("multiply_k", h, 0, 3), ("multiply_k", h, 1, 0), ("turn_k", h, 2, 1)]
+            pe += tiles("multiply_k", h, 1, 1, 3) + [("turn_k", h, 3, 0), ("multiply_k", h, 1, 3), ("turn_k", h, 3, 1)]
+            act += [("interleave_v", h, 1, 0)] + both("copy_k", h, 2)
             act += [("interleave_v", h, 1, 1)] + both("copy_k", h, 3)
             act += both("interleave_v", h, 2) + both("interleave_v", h, 3)
         else:
@@ -109,19 +118,21 @@ def engine_orders():
         dve += tiles("take_scores", h, 3, 0, 1) + values[:1] + tiles("take_scores", h, 3, 1, PACK)
         dve += [("invert_sum", h, 0), values[1]] + weigh[0] + [("invert_sum", h, 1), values[2]] + weigh[1]
         dve += [("invert_sum", h, 2)] + weave(parts("quantize_w", h, 0), weigh[2]) + [("invert_sum", h, 3)]
+        first_products = turn[0] + [("warm", 4 + 2 * h, 2), turn[1][0], ("warm", 5 + 2 * h, 2), turn[1][1]]
+        first_products += weave(parts("multiply_v", h, 0), turn[2])
         if not last:
-            pe += turn[0] + [("offsets", h + 1)] + turn[1] + weave(parts("multiply_v", h, 0), turn[2])
+            pe += [("offsets", h + 1, 0, PACK)] + first_products
             pe += both("turn_k", h + 1, 0) + parts("multiply_v", h, 1) + both("turn_k", h + 1, 1) + turn[3]
             next_q = [("copy_q", h + 1) + part for part in q_parts(h + 1)]
             act += [next_q[0], bias[0], exp[0], bias[1], next_q[1], exp[1], bias[2], bias[3], exp[2]]
-            act += copy[0] + [("copy_offsets", h + 1), exp[3]] + copy[1] + [("store_result", h, 0, 0)]
+            act += copy[0] + [("copy_offsets", h + 1, 0, PACK), exp[3]] + copy[1] + [("store_result", h, 0, 0)]
             act += both("copy_k", h + 1, 0) + copy[2] + [("store_result", h, 1, 0)] + both("copy_k", h + 1, 1)
             act += copy[3] + [("interleave_v", h + 1, 0, 0)]
             second = parts("quantize_w", h, 1)
             dve += [("scale_q", h + 1, 0, 0, PACK), second[0], weigh[3][0], second[1]]
-            dve += [("quantize_qk", h + 1, 0), weigh[3][1]] + parts("quantize_w", h, 2)
+            dve += [("quantize_qk", h + 1, 0), weigh[3][1]] + parts("quantize_w", h, 2) + [("scale_q", h + 1, 1, 0, PACK)]
         else:
-            pe += turn[0] + [("warm", 3, 2), turn[1][0], ("warm", 4, 2), turn[1][1]] + weave(parts("multiply_v", h, 0), turn[2])
+            pe += first_products
             pe += parts("multiply_v", h, 1) + turn[3][:1] + parts("multiply_v", h, 2) + turn[3][1:] + parts("multiply_v", h, 3)
             act += [bias[0], exp[0], bias[1], bias[2], exp[1], bias[3], exp[2]]
             act += copy[0] + [exp[3]] + copy[1] + copy[2] + [("store_result", h, 0, 0)]
@@ -140,14 +151,15 @@ def producers(step):
         "copy_factors": lambda: [("turn_factors",)],
         "copy_q": lambda h, i0, i1: [("turn_q", h, i0, i1)],
         "copy_k": lambda h, g, b: [("turn_k", h, g, b)],
-        "offsets": lambda h: [("copy_factors",)] + [("copy_q", h) + part for part in q_parts(h)],
-        "copy_offsets": lambda h: [("offsets", h)],
+        "offsets": lambda h, i0, i1: [("copy_factors",)] + [("copy_q", h) + part for part in q_parts(h) if i0 <= part[0] < i1],
+        "copy_offsets": lambda h, i0, i1: [("offsets", h, i0, i1)],
         "scale_q": lambda h, g, i0, i1: [("copy_factors",)] + [("copy_q", h) + part for part in q_parts(h) if i0 <= part[0] < i1],
         "quantize_qk": lambda h, g: [("scale_q", h, g, PACK - 1 if (h, g) == (0, 0) else 0, PACK)]
         + [("copy_k", h, g, b) for b in HALVES],
         "quantize_v": lambda h, g0, g1: [("interleave_v", h, g, b) for g in range(g0, g1) for b in HALVES],
         "multiply_k": lambda h, g, i: [("quantize_qk", h, g)],
-        "take_scores": lambda h, g, i: [("multiply_k", h, g, i), ("copy_offsets", h)],
+        "take_scores": lambda h, g, i: [("multiply_k", h, g, i)]
+        + [("copy_offsets", h) + part for part in offset_parts(h) if part[0] <= i < part[1]],
         "exp_bias": lambda h, i: [("take_scores", h, G - 1, i)],
         "exponentiate": lambda h, i: [("exp_bias", h, i)],
         "invert_sum": lambda h, i: [("exponentiate", h, i)],
@@ -293,7 +305,7 @@ def tile_kivigroupedscalefoldedattention_x1_kernel(tc, q, k_code, k_scale, k_zer
             )
 
         def warm(number, count):
-            idle_bank = bank_tile(SCORE_BANKS - 1 if number < 3 else RESULT_BANK, [P, W], F32)
+            idle_bank = bank_tile(SCORE_BANKS - 1 if number < 4 else RESULT_BANK, [P, W], F32)
             for repeat in range(count):
                 nc.tensor.matmul(idle_bank[:], lhsT=zeros[:, 0:P], rhs=zeros[:], start=True, stop=True)
 
@@ -327,22 +339,22 @@ def tile_kivigroupedscalefoldedattention_x1_kernel(tc, q, k_code, k_scale, k_zer
             dst = as_words(qk_tile(h, g)[:, N + 2 * P * u : N + 2 * P * (u + 1), :]).rearrange("p (m e w) -> p m e w", e=2, w=2)
             nc.scalar.copy(out=dst, in_=live["k", h, g, u][:].rearrange("p e w m -> p m e w"))
 
-        def offsets(h):
-            bank = bank_tile(RESULT_BANK, [P, PACK, G], F32)
+        def offsets(h, i0, i1):
+            bank = bank_tile(RESULT_BANK if h == 0 else 0, [P, i1 - i0, G], F32)
             zero_rows = slice(rows + h * G, rows + (h + 1) * G)
-            for i in range(PACK):
+            for i in range(i0, i1):
                 for j in range(PACK):
                     nc.tensor.matmul(
-                        bank[:, i, :],
+                        bank[:, i - i0, :],
                         lhsT=q_turned[h][:, i * P : (i + 1) * P, j],
                         rhs=factors[:, zero_rows, j],
                         start=(j == 0),
                         stop=(j == PACK - 1),
                     )
-            live["off", h] = bank
+            live["off", h, i0] = bank
 
-        def copy_offsets(h):
-            nc.scalar.copy(out=off[h][:], in_=live["off", h][:])
+        def copy_offsets(h, i0, i1):
+            nc.scalar.copy(out=off[h][:, i0:i1, :], in_=live["off", h, i0][:])
 
         def scale_q(h, g, i0, i1):
             cols = slice(i0 * P, i1 * P)

from contextlib import ExitStack

import concourse.mybir as mybir
from concourse.masks import make_identity

H, N, G, T, D = 2, 512, 4, 2048, 512
FLOPS = 2 * 2 * H * N * T * D

F32 = mybir.dt.float32
BF16 = mybir.dt.bfloat16
I32 = mybir.dt.int32
U32 = mybir.dt.uint32
U8 = mybir.dt.uint8
FP8X4 = mybir.dt.float8_e4m3fn_x4
ALU = mybir.AluOpType
ACT = mybir.ActivationFunctionType

P = 128
PACK = 4
W = T // G
SOFTMAX_SCALE = D**-0.5
HALVES = (0, 1)
LAST_TILE = (H - 1, PACK - 1)

TRANSPOSE_BANKS = 4
SCORE_BANKS = 3
V_SCALE_BANK = 1
RESULT_BANK = 3


def q_parts(h):
    return [(i, i + 1) for i in range(PACK)] if h == 0 else [(0, 2), (2, 4)]


def offset_parts(h):
    return [(0, 2), (2, 4)] if h == 0 else [(0, PACK)]


def weight_parts(h, i):
    return [(0, 2), (2, 3), (3, 4)] if (h, i) == LAST_TILE else [(0, 2), (2, 4)]


def product_parts(h, i):
    return weight_parts(h, i) if i < 2 or (h, i) == LAST_TILE else [(0, G)]


def value_parts():
    return [(0, 2), (2, 3), (3, 4)]


def channel_parts(split):
    return [slice(c * D // 2, (c + 1) * D // 2) for c in HALVES] if split else [slice(0, D)]


def engine_orders():
    pe, act, dve = [], [], []

    def both(name, h, g):
        return [(name, h, g, b) for b in HALVES]

    def parts(name, h, i):
        split = product_parts if name in ("quantize_w", "multiply_v") else weight_parts
        return [(name, h, i) + part for part in split(h, i)]

    def tiles(name, h, g, first, end):
        return [(name, h, g, i) for i in range(first, end)]

    def weave(first, second):
        return [step for pair in zip(first, second) for step in pair]

    first_q = [("turn_q", 0) + part for part in q_parts(0)]
    pe += [("warm", 0, 3), first_q[0], ("turn_factors",)] + first_q[1:]
    pe += [("warm", 1, 2)] + both("turn_k", 0, 0) + [("warm", 2, 2)] + both("turn_k", 0, 1)
    pe += [("warm", 3, 2), ("offsets", 0, 0, 2)] + tiles("multiply_k", 0, 0, 0, 2) + [("offsets", 0, 2, 4), ("multiply_k", 0, 0, 2)]
    act += [("copy_q", 0) + part for part in q_parts(0)] + both("copy_k", 0, 0)
    act += [("interleave_v", 0, 0, 0)] + both("copy_k", 0, 1)
    act += [("copy_offsets", 0, 0, 2), ("interleave_v", 0, 0, 1), ("copy_offsets", 0, 2, 4)]
    dve += [("copy_factors",)] + [("scale_q", 0, 0) + part for part in q_parts(0)]
    dve += [("scale_q", 0, 1, 0, PACK), ("scale_q", 0, 2, 0, PACK), ("quantize_qk", 0, 0), ("scale_q", 0, 3, 0, PACK)]
    dve += [("quantize_qk", 0, 1)]

    for h in range(H):
        first, last = h == 0, h == H - 1

        for g in range(G - 1):
            if not first and g + 2 < G:
                dve += [("scale_q", h, g + 2, 0, PACK)]
            dve += tiles("take_scores", h, g, 0, 2)
            if not first and g == 0:
                dve += parts("quantize_w", h - 1, 3)
            if (h, g) != (0, 0):
                dve += [("quantize_qk", h, g + 1)]
            dve += tiles("take_scores", h, g, 2, PACK)
        if first:
            pe += [("turn_k", h, 2, 0), ("multiply_k", h, 0, 3), ("multiply_k", h, 1, 0), ("turn_k", h, 2, 1)]
            pe += tiles("multiply_k", h, 1, 1, 3) + [("turn_k", h, 3, 0), ("multiply_k", h, 1, 3), ("turn_k", h, 3, 1)]
            act += [("interleave_v", h, 1, 0)] + both("copy_k", h, 2)
            act += [("interleave_v", h, 1, 1)] + both("copy_k", h, 3)
            act += both("interleave_v", h, 2) + both("interleave_v", h, 3)
        else:
            pe += tiles("multiply_k", h, 0, 0, 3) + [("turn_k", h, 2, 0)] + parts("multiply_v", h - 1, 2)
            pe += [("multiply_k", h, 0, 3), ("turn_k", h, 2, 1)]
            pe += tiles("multiply_k", h, 1, 0, 3) + parts("multiply_v", h - 1, 3) + [("multiply_k", h, 1, 3)] + both("turn_k", h, 3)
            act += [("copy_k", h, 2, 0), ("interleave_v", h, 0, 1), ("store_result", h - 1, 2, 0), ("copy_k", h, 2, 1)]
            act += both("interleave_v", h, 1) + [("store_result", h - 1, 3, 0), ("interleave_v", h, 2, 0)] + both("copy_k", h, 3)
            act += [("interleave_v", h, 2, 1)] + both("interleave_v", h, 3)
        pe += tiles("multiply_k", h, 2, 0, PACK)
        if not last:
            pe += [("turn_q", h + 1) + part for part in q_parts(h + 1)]
        pe += tiles("multiply_k", h, 3, 0, PACK) + [("spread_v_scale", h, b) for b in HALVES]

        values = [("quantize_v", h) + part for part in value_parts()]
        weigh = [parts("weigh", h, i) for i in range(PACK)]
        turn = [parts("turn_w", h, i) for i in range(PACK)]
        copy = [parts("copy_w", h, i) for i in range(PACK)]
        bias = [("exp_bias", h, i) for i in range(PACK)]
        exp = [("exponentiate", h, i) for i in range(PACK)]
        dve += tiles("take_scores", h, 3, 0, 1) + values[:1] + tiles("take_scores", h, 3, 1, PACK)
        dve += [("invert_sum", h, 0), values[1]] + weigh[0] + [("invert_sum", h, 1), values[2]] + weigh[1]
        dve += [("invert_sum", h, 2)] + weave(parts("quantize_w", h, 0), weigh[2]) + [("invert_sum", h, 3)]
        first_products = turn[0] + [("warm", 4 + 2 * h, 2), turn[1][0], ("warm", 5 + 2 * h, 2), turn[1][1]]
        first_products += weave(parts("multiply_v", h, 0), turn[2])
        if not last:
            pe += [("offsets", h + 1, 0, PACK)] + first_products
            pe += both("turn_k", h + 1, 0) + parts("multiply_v", h, 1) + both("turn_k", h + 1, 1) + turn[3]
            next_q = [("copy_q", h + 1) + part for part in q_parts(h + 1)]
            act += [next_q[0], bias[0], exp[0], bias[1], next_q[1], exp[1], bias[2], bias[3], exp[2]]
            act += copy[0] + [("copy_offsets", h + 1, 0, PACK), exp[3]] + copy[1] + [("store_result", h, 0, 0)]
            act += both("copy_k", h + 1, 0) + copy[2] + [("store_result", h, 1, 0)] + both("copy_k", h + 1, 1)
            act += copy[3] + [("interleave_v", h + 1, 0, 0)]
            second = parts("quantize_w", h, 1)
            dve += [("scale_q", h + 1, 0, 0, PACK), second[0], weigh[3][0], second[1]]
            dve += [("quantize_qk", h + 1, 0), weigh[3][1]] + parts("quantize_w", h, 2) + [("scale_q", h + 1, 1, 0, PACK)]
        else:
            pe += first_products
            pe += parts("multiply_v", h, 1) + turn[3][:1] + parts("multiply_v", h, 2) + turn[3][1:] + parts("multiply_v", h, 3)
            act += [bias[0], exp[0], bias[1], bias[2], exp[1], bias[3], exp[2]]
            act += copy[0] + [exp[3]] + copy[1] + copy[2] + [("store_result", h, 0, 0)]
            act += copy[3][:1] + [("store_result", h, 1, 0)] + copy[3][1:] + [("store_result", h, 2, 0)]
            act += both("store_result", h, 3)
            final = parts("quantize_w", h, 3)
            dve += parts("quantize_w", h, 1) + weigh[3][:1] + parts("quantize_w", h, 2) + weigh[3][1:]
            dve += [final[0], ("round_result", h - 1, 0)] + final[1:] + [("round_result", h - 1, 1), ("store_planes", h - 1, 0)]
            dve += [("round_result", h, c) for c in HALVES] + [("store_planes", h, c) for c in HALVES]
    return pe, act, dve


def producers(step):
    name, args = step[0], step[1:]
    table = {
        "copy_factors": lambda: [("turn_factors",)],
        "copy_q": lambda h, i0, i1: [("turn_q", h, i0, i1)],
        "copy_k": lambda h, g, b: [("turn_k", h, g, b)],
        "offsets": lambda h, i0, i1: [("copy_factors",)] + [("copy_q", h) + part for part in q_parts(h) if i0 <= part[0] < i1],
        "copy_offsets": lambda h, i0, i1: [("offsets", h, i0, i1)],
        "scale_q": lambda h, g, i0, i1: [("copy_factors",)] + [("copy_q", h) + part for part in q_parts(h) if i0 <= part[0] < i1],
        "quantize_qk": lambda h, g: [("scale_q", h, g, PACK - 1 if (h, g) == (0, 0) else 0, PACK)]
        + [("copy_k", h, g, b) for b in HALVES],
        "quantize_v": lambda h, g0, g1: [("interleave_v", h, g, b) for g in range(g0, g1) for b in HALVES],
        "multiply_k": lambda h, g, i: [("quantize_qk", h, g)],
        "take_scores": lambda h, g, i: [("multiply_k", h, g, i)]
        + [("copy_offsets", h) + part for part in offset_parts(h) if part[0] <= i < part[1]],
        "exp_bias": lambda h, i: [("take_scores", h, G - 1, i)],
        "exponentiate": lambda h, i: [("exp_bias", h, i)],
        "invert_sum": lambda h, i: [("exponentiate", h, i)],
        "weigh": lambda h, i, g0, g1: [("invert_sum", h, i), ("spread_v_scale", h, g0 // 2)],
        "turn_w": lambda h, i, g0, g1: [("weigh", h, i, g0, g1)],
        "copy_w": lambda h, i, g0, g1: [("turn_w", h, i, g0, g1)],
        "quantize_w": lambda h, i, g0, g1: [("copy_w", h, i) + part for part in weight_parts(h, i) if g0 <= part[0] < g1],
        "multiply_v": lambda h, i, g0, g1: [("quantize_w", h, i, g0, g1)] + [("quantize_v", h) + part for part in value_parts()],
        "store_result": lambda h, i, c: [("multiply_v", h, i) + product_parts(h, i)[-1]],
        "round_result": lambda h, c: [("store_result", h, i, c if (h, i) == LAST_TILE else 0) for i in range(PACK)],
        "store_planes": lambda h, c: [("round_result", h, c)] if h == H - 1 else [("round_result", h, b) for b in HALVES],
    }
    return table[name](*args) if name in table else []


def schedule():
    queues = [list(order) for order in engine_orders()]
    written, text = set(), []
    for place in range(sum(len(order) for order in queues)):
        ready = [order for order in queues if order and all(p in written for p in producers(order[0]))]
        step = ready[0][0]
        ready[0].remove(step)
        written.add(step)
        text.append(step)
    return text


def tile_kivigroupedscalefoldedattention_x1_kernel(tc, q, k_code, k_scale, k_zero, v_code, v_scale, out_0, out_1, out_2):
    nc = tc.nc
    with ExitStack() as ctx:
        sbuf = ctx.enter_context(tc.tile_pool(name="sbuf", bufs=1))
        banks = ctx.enter_context(tc.psum_pool(name="banks", bufs=1))
        turn_banks = ctx.enter_context(tc.psum_pool(name="turn", bufs=TRANSPOSE_BANKS))
        ctx.enter_context(tc.manual_schedule())

        def rotating(tag, bufs, shape, dtype):
            return sbuf.tile(shape, dtype, name=tag, tag=tag, bufs=bufs, align_bytes=64)

        def kept(name, shape, dtype):
            return rotating(name, 1, shape, dtype)

        def staged(tag, shape, dtype):
            return rotating(tag, 3, shape, dtype)

        def per_head(tag, shape, dtype):
            return rotating(tag, 4, shape, dtype)

        def bank_tile(number, shape, dtype):
            return banks.tile(shape, dtype, name="bank%d" % number, tag="bank%d" % number)

        rows = H * G
        factor_rows = kept("factor_rows", [P, D], BF16)
        nc.gpsimd.memset(factor_rows[:].bitcast(I32), 0)
        nc.scalar.dma_start(out=factor_rows[0:rows, :], in_=k_scale.rearrange("h g d -> (h g) d"))
        nc.scalar.dma_start(out=factor_rows[rows : 2 * rows, :], in_=k_zero.rearrange("h g d -> (h g) d"))
        nc.scalar.dma_start(out=factor_rows[2 * rows : 3 * rows, :], in_=v_scale.rearrange("h (g t) -> (h g) t", g=G))
        ident = kept("ident", [P, P], F32)
        make_identity(nc, ident[:])
        pick = kept("pick", [P, rows], BF16)
        nc.gpsimd.tensor_copy(out=pick[:], in_=ident[:, 2 * rows : 3 * rows])
        exp_warm = kept("exp_warm", [P, 1], F32)
        nc.scalar.activation(out=exp_warm[:], in_=ident[:, 0:1], func=ACT.Exp)

        q_rows, k_rows, v_rows = {}, {}, {}

        def load_q(h):
            src = q[h].rearrange("(p j) d -> p j d", j=PACK)
            for i0, i1 in q_parts(h):
                q_rows[h, i0] = kept("q_rows%d%d" % (h, i0), [P, i1 - i0, D], BF16)
                nc.sync.dma_start(out=q_rows[h, i0][:], in_=src[:, i0:i1, :])

        def load_k(h, g):
            src = k_code[h, g].rearrange("(p j) d -> p j d", j=PACK)
            for u in HALVES:
                k_rows[h, g, u] = kept("k_rows%d%d%d" % (h, g, u), [P, 2, D], BF16)
                nc.sync.dma_start(out=k_rows[h, g, u][:], in_=src[:, 2 * u : 2 * u + 2, :])

        def load_v(h, g):
            v_rows[h, g] = per_head("v_rows", [P, PACK, D], BF16)
            nc.sync.dma_start(out=v_rows[h, g][:], in_=v_code[h, g * W : (g + 1) * W, :].rearrange("(p j) d -> p j d", j=PACK))

        load_q(0)
        load_k(0, 0)
        for h in range(H):
            for g in range(G):
                if g + 1 < G:
                    load_k(h, g + 1)
                load_v(h, g)
            if h + 1 < H:
                load_q(h + 1)
                load_k(h + 1, 0)

        factors = kept("factors", [P, 2 * rows, PACK], BF16)
        q_turned = {h: kept("q_turned%d" % h, [P, N, PACK], BF16) for h in range(H)}
        off = {h: kept("off%d" % h, [P, PACK, G], F32) for h in range(H)}
        run_max = {h: kept("run_max%d" % h, [P, PACK, G], F32) for h in range(H)}
        neg_max = {h: kept("neg_max%d" % h, [P, PACK], F32) for h in range(H)}
        row_sum = {h: kept("row_sum%d" % h, [P, PACK], F32) for h in range(H)}
        row_inv = {h: kept("row_inv%d" % h, [P, PACK], F32) for h in range(H)}
        result = {h: kept("result%d" % h, [P, PACK, D], F32) for h in range(H)}
        rounded = {h: kept("rounded%d" % h, [P, D, PACK], BF16) for h in range(H)}
        out_codes = kept("out_codes", [P, H * D], U32)
        out_scales = kept("out_scales", [P, H * D], U8)
        zeros = kept("zeros", [P, W], BF16)
        nc.vector.memset(zeros[:].bitcast(I32), 0)
        live = {}

        def as_words(packed):
            return packed.rearrange("p c j -> p (c j)").bitcast(F32)

        def turn(key, sources, alternate):
            bank = turn_banks.tile([P, len(sources), 2, P], F32, name="turn_bank", tag="turn_bank")
            for r, source in enumerate(sources):
                words = source.bitcast(F32)
                for u in HALVES:
                    chosen = words[:, u : 2 * P : 2] if alternate else words[:, u * P : (u + 1) * P]
                    nc.tensor.transpose(bank[:, r, u, :], chosen, ident[:])
            live[key] = bank

        def copy_turned(key, packed):
            dst = as_words(packed).rearrange("p (r m u) -> p r m u", m=P, u=2)
            nc.scalar.copy(out=dst, in_=live[key][:].rearrange("p r u m -> p r m u"))

        def interleave(copy, packed, source):
            copy(out=packed.rearrange("p (c i) j -> p c j i", i=4), in_=source.rearrange("p j (c i) -> p c j i", i=4))

        def quantize(codes, scales, packed):
            nc.vector.quantize_mx(out=codes.bitcast(FP8X4), scales=scales, in_=packed.rearrange("p c j -> p (c j)"))

        def quantize_new(key, make_tile, tag, packed):
            live[key] = (make_tile(tag + "_codes", [P, packed.shape[1]], U32), make_tile(tag + "_scales", [P, packed.shape[1]], U8))
            quantize(live[key][0][:], live[key][1][:], packed)

        def multiply(out, stationary, stationary_cols, moving, moving_cols, start, stop):
            nc.tensor.matmul_mx(
                out=out,
                lhsT=stationary[0][:, stationary_cols].bitcast(FP8X4),
                lhsT_scale=stationary[1][:, stationary_cols],
                rhs=moving[0][:, moving_cols].bitcast(FP8X4),
                rhs_scale=moving[1][:, moving_cols],
                start=start,
                stop=stop,
            )

        def warm(number, count):
            idle_bank = bank_tile(SCORE_BANKS - 1 if number < 4 else RESULT_BANK, [P, W], F32)
            for repeat in range(count):
                nc.tensor.matmul(idle_bank[:], lhsT=zeros[:, 0:P], rhs=zeros[:], start=True, stop=True)

        def turn_factors():
            bank = bank_tile(RESULT_BANK, [P, 2, P], F32)
            for u in HALVES:
                nc.tensor.transpose(bank[:, u, :], factor_rows[:].bitcast(F32)[:, u : 2 * P : 2], ident[:])
            live["factors"] = bank

        def copy_factors():
            nc.vector.tensor_copy(
                out=as_words(factors[:]).rearrange("p (r u) -> p r u", u=2),
                in_=live["factors"][:, :, 0 : 2 * rows].rearrange("p u r -> p r u"),
            )

        def turn_q(h, i0, i1):
            turn(("q", h, i0), [q_rows[h, i0][:, r, :] for r in range(i1 - i0)], True)

        def copy_q(h, i0, i1):
            copy_turned(("q", h, i0), q_turned[h][:, P * i0 : P * i1, :])

        def qk_tile(h, g):
            if ("qk", h, g) not in live:
                live["qk", h, g] = per_head("qk", [P, N + W, PACK], BF16)
            return live["qk", h, g]

        def turn_k(h, g, u):
            turn(("k", h, g, u), [k_rows[h, g, u][:, e, :] for e in HALVES], True)

        def copy_k(h, g, u):
            dst = as_words(qk_tile(h, g)[:, N + 2 * P * u : N + 2 * P * (u + 1), :]).rearrange("p (m e w) -> p m e w", e=2, w=2)
            nc.scalar.copy(out=dst, in_=live["k", h, g, u][:].rearrange("p e w m -> p m e w"))

        def offsets(h, i0, i1):
            bank = bank_tile(RESULT_BANK if h == 0 else 0, [P, i1 - i0, G], F32)
            zero_rows = slice(rows + h * G, rows + (h + 1) * G)
            for i in range(i0, i1):
                for j in range(PACK):
                    nc.tensor.matmul(
                        bank[:, i - i0, :],
                        lhsT=q_turned[h][:, i * P : (i + 1) * P, j],
                        rhs=factors[:, zero_rows, j],
                        start=(j == 0),
                        stop=(j == PACK - 1),
                    )
            live["off", h, i0] = bank

        def copy_offsets(h, i0, i1):
            nc.scalar.copy(out=off[h][:, i0:i1, :], in_=live["off", h, i0][:])

        def scale_q(h, g, i0, i1):
            cols = slice(i0 * P, i1 * P)
            factor = factors[:, h * G + g : h * G + g + 1, :].to_broadcast([P, (i1 - i0) * P, PACK])
            nc.vector.tensor_tensor(out=qk_tile(h, g)[:, cols, :], in0=q_turned[h][:, cols, :], in1=factor, op=ALU.mult)

        def quantize_qk(h, g):
            quantize_new(("qk_mx", h, g), staged, "qk", qk_tile(h, g)[:])

        def interleave_v(h, g, c):
            g0, g1 = [part for part in value_parts() if part[0] <= g < part[1]][0]
            if (g, c) == (g0, 0):
                live["v", h, g0] = kept("v_packed%d" % g0, [P, (g1 - g0) * D, PACK], BF16)
            cols = channel_parts(True)[c]
            first = (g - g0) * D
            interleave(nc.scalar.copy, live["v", h, g0][:, first + cols.start : first + cols.stop, :], v_rows[h, g][:, :, cols])

        def quantize_v(h, g0, g1):
            quantize_new(("v_mx", h, g0), kept, "v%d" % g0, live["v", h, g0][:])

        def multiply_k(h, g, i):
            bank = bank_tile((g * PACK + i) % SCORE_BANKS, [P, W], F32)
            operands = live["qk_mx", h, g]
            multiply(bank[:], operands, slice(i * P, (i + 1) * P), operands, slice(N, N + W), True, True)
            live["scores_bank", h, g, i] = bank

        def take_scores(h, g, i):
            if g == 0:
                live["scores", h, i] = per_head("scores", [P, T], F32)
            nc.vector.tensor_scalar(
                out=live["scores", h, i][:, g * W : (g + 1) * W],
                in0=live["scores_bank", h, g, i][:],
                scalar1=off[h][:, i, g : g + 1],
                scalar2=run_max[h][:, i, g - 1 : g] if g > 0 else None,
                op0=ALU.add,
                op1=ALU.max,
                accum_out=run_max[h][:, i, g : g + 1],
            )

        def exp_bias(h, i):
            nc.scalar.activation(out=neg_max[h][:, i : i + 1], in_=run_max[h][:, i, G - 1 : G], func=ACT.Copy, scale=-SOFTMAX_SCALE)

        def exponentiate(h, i):
            nc.scalar.activation(
                out=live["scores", h, i][:],
                in_=live["scores", h, i][:],
                func=ACT.Exp,
                bias=neg_max[h][:, i : i + 1],
                scale=SOFTMAX_SCALE,
                accum_out=row_sum[h][:, i : i + 1],
            )

        def invert_sum(h, i):
            nc.vector.reciprocal(out=row_inv[h][:, i : i + 1], in_=row_sum[h][:, i : i + 1])

        def spread_v_scale(h, b):
            bank = bank_tile(V_SCALE_BANK + b, [P, 2, W], BF16)
            for r in HALVES:
                row = h * G + 2 * b + r
                nc.tensor.matmul(
                    bank[:, r, :],
                    lhsT=pick[:, row : row + 1].to_broadcast([P, P]),
                    rhs=factor_rows[:].rearrange("p (m u e) -> p u m e", u=2, e=2),
                    start=True,
                    stop=True,
                )
            live["v_scale", h, b] = bank

        def weigh(h, i, g0, g1):
            ws = per_head("ws", [P, (g1 - g0) * W], BF16)
            nc.vector.scalar_tensor_tensor(
                out=ws[:],
                in0=live["scores", h, i][:, g0 * W : g1 * W],
                scalar=row_inv[h][:, i : i + 1],
                in1=live["v_scale", h, g0 // 2][:, g0 % 2 : g0 % 2 + g1 - g0, :].rearrange("p r t -> p (r t)"),
                op0=ALU.mult,
                op1=ALU.mult,
            )
            live["ws", h, i, g0] = ws

        def turn_w(h, i, g0, g1):
            turn(("w", h, i, g0), [live["ws", h, i, g0][:, r * W : (r + 1) * W] for r in range(g1 - g0)], False)

        def copy_w(h, i, g0, g1):
            c0, c1 = [part for part in product_parts(h, i) if part[0] <= g0 < part[1]][0]
            if g0 == c0:
                live["w_packed", h, i, c0] = staged("w_packed", [P, (c1 - c0) * P, PACK], BF16)
            copy_turned(("w", h, i, g0), live["w_packed", h, i, c0][:, (g0 - c0) * P : (g1 - c0) * P, :])

        def quantize_w(h, i, g0, g1):
            quantize_new(("w_mx", h, i, g0), per_head, "w", live["w_packed", h, i, g0][:])

        def multiply_v(h, i, g0, g1):
            for c, cols in enumerate(channel_parts((h, i) == LAST_TILE)):
                if g0 == 0:
                    number = c if h == H - 1 and i % 2 else RESULT_BANK
                    live["result_bank", h, i, c] = bank_tile(number, [P, cols.stop - cols.start], F32)
                for g in range(g0, g1):
                    v0 = [part[0] for part in value_parts() if part[0] <= g < part[1]][0]
                    v_cols = slice((g - v0) * D + cols.start, (g - v0) * D + cols.stop)
                    w_cols = slice((g - g0) * P, (g - g0 + 1) * P)
                    multiply(live["result_bank", h, i, c][:], live["w_mx", h, i, g0], w_cols, live["v_mx", h, v0], v_cols, g == 0, g == G - 1)

        def store_result(h, i, c):
            split = channel_parts((h, i) == LAST_TILE)
            nc.scalar.copy(out=result[h][:, i, split[c]], in_=live["result_bank", h, i, c][:])
            if c == len(split) - 1:
                nc.sync.dma_start(out=out_0[h].rearrange("(p j) d -> p j d", j=PACK)[:, i, :], in_=result[h][:, i, :])

        def round_result(h, c):
            cols = channel_parts(True)[c]
            interleave(nc.vector.tensor_copy, rounded[h][:, cols, :], result[h][:, :, cols])

        def store_planes(h, c):
            cols = channel_parts(h == H - 1)[c]
            plane_cols = slice(h * D + cols.start, h * D + cols.stop)
            quantize(out_codes[:, plane_cols], out_scales[:, plane_cols], rounded[h][:, cols, :])
            out_words = out_1[0].rearrange("p m t -> p (m t)").bitcast(I32)
            nc.sync.dma_start(out=out_words[:, plane_cols], in_=out_codes[:, plane_cols].bitcast(I32))
            if plane_cols.stop == H * D:
                for a in range(4):
                    queue = nc.sync if a % 2 else nc.scalar
                    queue.dma_start(out=out_2[0, 4 * a : 4 * a + 4, :].bitcast(I32), in_=out_scales[32 * a : 32 * a + 4, :].bitcast(I32))

        steps = {
            "warm": warm, "turn_factors": turn_factors, "copy_factors": copy_factors, "turn_q": turn_q, "copy_q": copy_q,
            "turn_k": turn_k, "copy_k": copy_k, "offsets": offsets, "copy_offsets": copy_offsets, "scale_q": scale_q,
            "quantize_qk": quantize_qk, "interleave_v": interleave_v, "quantize_v": quantize_v, "multiply_k": multiply_k,
            "take_scores": take_scores, "exp_bias": exp_bias, "exponentiate": exponentiate, "invert_sum": invert_sum,
            "spread_v_scale": spread_v_scale, "weigh": weigh, "turn_w": turn_w, "copy_w": copy_w, "quantize_w": quantize_w,
            "multiply_v": multiply_v, "store_result": store_result, "round_result": round_result, "store_planes": store_planes,
        }
        for step in schedule():
            steps[step[0]](*step[1:])
